import numpy as np
import ml_dtypes


def mxq(x, axis, fmt="e4m3"):
    dtype, down = {"e4m3": (ml_dtypes.float8_e4m3fn, 7), "e5m2": (ml_dtypes.float8_e5m2, 14)}[fmt]
    v = np.moveaxis(np.asarray(x, np.float32).astype(ml_dtypes.bfloat16).astype(np.float64), axis, -1)
    blocks = v.reshape(v.shape[:-1] + (-1, 32))
    amax = np.abs(blocks).max(-1, keepdims=True)
    byte = np.maximum(np.where(amax > 0, np.frexp(amax)[1] - 1 + 127, 0) - down, 1)
    scale = np.exp2(byte - 127.0)
    codes = (blocks / scale).astype(np.float32).astype(dtype).astype(np.float64)
    return np.moveaxis((codes * scale).reshape(v.shape), -1, axis)


WIDE = False


def mx_kscale(k):
    if not WIDE:
        return np.ones(k)
    levels = np.array([24, -24, 12, -12, 0])
    if k % 512:
        return np.exp2(np.random.permutation(np.resize(levels, k // 32))).repeat(32)
    a = np.empty((k // 512, 16))
    for p in range(k // 512):
        a[p, :8] = np.random.permutation(np.resize(levels, 8))
        for g in range(8):
            far = levels[np.abs(levels - a[p, g]) >= 10]
            a[p, g + 8] = far[np.random.randint(len(far))]
    return np.exp2(a.ravel()).repeat(32)


def f64(x):
    return np.asarray(x).astype(np.float64)


def striped(idx):
    return np.tile(idx.reshape(-1, 16).T, (8, 1)).astype(np.uint16)


def unstriped(offs):
    return offs[:16].T.reshape(-1).astype(np.int64)


E2M1 = np.array([0.0, 0.5, 1.0, 1.5, 2.0, 3.0, 4.0, 6.0, -0.0, -0.5, -1.0, -1.5, -2.0, -3.0, -4.0, -6.0])


def pack_weight(w, fmt):
    k, n = w.shape
    w = f64(np.asarray(w, np.float32).astype(ml_dtypes.bfloat16)).reshape(k // 32, 32, n)
    amax = np.abs(w).max(1)
    if fmt == "e4m3":
        byte = np.frexp(amax)[1] - 1 + 127 - 7
    else:
        mant, ex = np.frexp(amax / 6.0)
        byte = np.where(mant > 0.5, ex, ex - 1) + 127
    byte = np.clip(np.where(amax > 0, byte, 1), 1, 254)
    scaled = (w * np.exp2(127.0 - byte)[:, None, :]).reshape(k, n).astype(np.float32)
    by_word = np.ascontiguousarray(scaled.reshape(k // 512, 128, 4, n).transpose(0, 1, 3, 2))
    if fmt == "e4m3":
        words = by_word.astype(ml_dtypes.float8_e4m3fn).view(np.uint8)
    else:
        c = by_word.astype(ml_dtypes.float4_e2m1fn).view(np.uint8) & 0xF
        words = (c[..., 0::2] | (c[..., 1::2] << 4)).reshape(k // 512, 128, 2 * n)
    return np.ascontiguousarray(words), np.ascontiguousarray(byte.astype(np.uint8).reshape(k // 512, 16, n))


def unpack_weight(words, scales, fmt):
    g, _, n = scales.shape
    words = np.ascontiguousarray(words).reshape(g, 128, n, -1)
    if fmt == "e4m3":
        vals = words.view(ml_dtypes.float8_e4m3fn).astype(np.float64)
    else:
        nib = np.empty((g, 128, n, 4), np.uint8)
        nib[..., 0::2] = words & 0xF
        nib[..., 1::2] = words >> 4
        vals = E2M1[nib]
    vals = vals * np.repeat(np.exp2(scales.astype(np.float64) - 127.0), 8, axis=1)[..., None]
    return vals.transpose(0, 1, 3, 2).reshape(g * 512, n)


def silu(f):
    return f / (1.0 + np.exp(-np.maximum(f, -700.0)))


def sigm(f):
    return 1.0 / (1.0 + np.exp(-np.maximum(f, -700.0)))


K, N, T, J = 1536, 256, 4096, 1024


def setup_inputs():
    n = np.random.standard_normal
    s = mx_kscale(K)[:, None]
    p_tab = pack_weight(n((K, T)) * s, "e4m3")
    p_wg = pack_weight(n((K, N)) / np.sqrt(K) / s, "e2m1")
    p_wh4 = pack_weight(n((K, N)) / np.sqrt(K) / s, "e2m1")
    return {
        "tab_words": p_tab[0],
        "tab_scales": p_tab[1],
        "wg_words": p_wg[0],
        "wg_scales": p_wg[1],
        "wh4_words": p_wh4[0],
        "wh4_scales": p_wh4[1],
        "whd": (0.4 * (n((K, N)) / np.sqrt(K) / s)).astype(np.float32),
        "bg": (0.3 * n(N) - 1.0).astype(np.float32),
        "rT": (n((N, T))).astype(np.float32),
        "offs": striped(np.random.permutation(T)[:J]),
    }


def reference(tab_words, tab_scales, wg_words, wg_scales, wh4_words, wh4_scales, whd, bg, rT, offs):
    idx = unstriped(offs)
    tab_ = unpack_weight(tab_words, tab_scales, "e4m3")[:, idx]
    wg_ = unpack_weight(wg_words, wg_scales, "e2m1")
    wh4_ = unpack_weight(wh4_words, wh4_scales, "e2m1")
    whd_ = mxq(f64(whd), 0, "e4m3")
    ga = wg_.T @ tab_
    gate = sigm(ga + f64(bg)[:, None])
    ha = wh4_.T @ tab_ + whd_.T @ tab_
    return f64(rT)[:, idx] + gate * (silu(ha) - f64(rT)[:, idx])

@@ -1,0 +1,207 @@
+from contextlib import ExitStack
+
+import concourse.mybir as mybir
+
+K, N, T, J = 1536, 256, 4096, 1024
+FLOPS = 3 * 2 * K * N * J
+
+F32 = mybir.dt.float32
+BF16 = mybir.dt.bfloat16
+I32 = mybir.dt.int32
+U32 = mybir.dt.uint32
+U16 = mybir.dt.uint16
+U8 = mybir.dt.uint8
+FP8X4 = mybir.dt.float8_e4m3fn_x4
+FP4X4 = mybir.dt.float4_e2m1fn_x4
+ALU = mybir.AluOpType
+ACT = mybir.ActivationFunctionType
+
+P = 128
+PASSES = K // 512
+HALVES = N // P
+BANK = 512
+BANKS = J // BANK
+GROUP = 16
+STAGE_ROW0 = 4
+STAGE_STEP = 8
+TAB_BYTES = PASSES * J
+W_BYTES = PASSES * N
+PLANE_WORDS = (TAB_BYTES + 2 * W_BYTES) // 4
+EPILOGUE_CUTS = ((0, 512, 1024), (0, 256, 512, 768, 1024))
+
+
+def tile_list_hwayt_dl_silu_kernel(
+    tc, tab_words, tab_scales, wg_words, wg_scales, wh4_words, wh4_scales, whd, bg, rT, offs, out
+):
+    nc = tc.nc
+    staged_rows = slice(STAGE_ROW0, P, STAGE_STEP)
+
+    with ExitStack() as ctx:
+        keep = ctx.enter_context(tc.tile_pool(name="keep", bufs=1))
+        big = ctx.enter_context(tc.tile_pool(name="big", bufs=3))
+        psum = ctx.enter_context(tc.psum_pool(name="psum", bufs=1))
+
+        offsets = keep.tile([P, J // GROUP], U16, name="offsets")
+        nc.sync.dma_start(offsets[:], offs)
+
+        def listed(j0, j1):
+            return offsets[:, j0 // GROUP : j1 // GROUP]
+
+        scale_window = keep.tile([P, PASSES, T // 4], I32, name="scale_window", tag="reused", align_bytes=64)
+        nc.vector.memset(scale_window[:], 0)
+        planes = keep.tile([P, PLANE_WORDS], I32, name="planes", align_bytes=64)
+        nc.vector.memset(planes[:], 0)
+
+        staged = keep.tile([P, PLANE_WORDS], I32, name="staged", align_bytes=64)
+        for w, scales in enumerate((wg_scales, wh4_scales)):
+            c0 = (TAB_BYTES + w * W_BYTES) // 4
+            nc.sync.dma_start(
+                staged[staged_rows, c0 : c0 + W_BYTES // 4].rearrange("q (a n) -> q a n", a=PASSES),
+                scales.rearrange("a q n -> q a n").bitcast(I32),
+            )
+        nc.scalar.dma_start(
+            scale_window[staged_rows, :, :], tab_scales.rearrange("a q t -> q a t").bitcast(I32)
+        )
+
+        bias = keep.tile([P, HALVES], F32, name="bias")
+        with nc.allow_non_contiguous_dma(reason="one bias value for each partition"):
+            nc.gpsimd.dma_start(bias[:], bg.rearrange("(h p) -> p h", p=P))
+        neg_bias = keep.tile([P, HALVES], F32, name="neg_bias")
+        nc.gpsimd.tensor_scalar(neg_bias[:], bias[:], -1.0, 0.0, ALU.mult, ALU.add)
+
+        def load_table(a):
+            words = big.tile([P, T], I32, name=f"table{a}", tag="big", align_bytes=64)
+            nc.sync.dma_start(words[:], tab_words[a].rearrange("p t i -> p (t i)").bitcast(I32))
+            return words
+
+        tables = [load_table(0)]
+        fp4_words = []
+        for name, words in (("wg", wg_words), ("wh4", wh4_words)):
+            tile = keep.tile([P, PASSES, 2 * N], U8, name=name, align_bytes=64)
+            nc.sync.dma_start(tile[:].bitcast(I32), words.rearrange("a p n -> p a n").bitcast(I32))
+            fp4_words.append(tile)
+        tables += [load_table(a) for a in range(1, PASSES)]
+
+        picked_scales = keep.tile([P, PASSES, J], U8, name="picked_scales", align_bytes=64)
+        for a in range(PASSES):
+            nc.vector.tensor_copy(
+                picked_scales[:, a, :], scale_window[:, a, :].bitcast(U8).indirect(offsets[:])
+            )
+        nc.vector.tensor_copy(
+            staged[:, : TAB_BYTES // 4], picked_scales[:].rearrange("p a j -> p (a j)").bitcast(I32)
+        )
+        for r in range(4):
+            nc.scalar.dma_start(planes[r:P:32, :], staged[STAGE_ROW0 + STAGE_STEP * r : P : 32, :])
+        plane_bytes = planes[:].bitcast(U8)
+
+        gate_sum = [[psum.tile([P, BANK], F32, name=f"gate{h}{b}") for b in range(BANKS)] for h in range(HALVES)]
+        hidden_sum = [[psum.tile([P, BANK], F32, name=f"hid{h}{b}") for b in range(BANKS)] for h in range(HALVES)]
+
+        picked = keep.tile([P, PASSES, J], U32, name="picked", tag="reused", align_bytes=64)
+
+        def multiply(acc, lhsT, lhsT_scale, a, b, start, stop):
+            nc.tensor.matmul_mx(
+                out=acc[:],
+                lhsT=lhsT,
+                lhsT_scale=lhsT_scale,
+                rhs=picked[:, a, b * BANK : (b + 1) * BANK].bitcast(FP8X4),
+                rhs_scale=plane_bytes[:, a * J + b * BANK : a * J + (b + 1) * BANK],
+                start=start,
+                stop=stop,
+            )
+
+        def multiply_fp4(w, acc, a, h, b, start, stop):
+            c0 = TAB_BYTES + w * W_BYTES + a * N + h * P
+            codes = fp4_words[w][:, a, 2 * h * P : 2 * (h + 1) * P].bitcast(FP4X4)
+            multiply(acc, codes, plane_bytes[:, c0 : c0 + P], a, b, start, stop)
+
+        for a in range(PASSES):
+            for b in range(BANKS):
+                nc.vector.tensor_copy(
+                    picked[:, a, b * BANK : (b + 1) * BANK],
+                    tables[a][:].bitcast(U32).indirect(listed(b * BANK, (b + 1) * BANK)),
+                )
+            for b in range(BANKS):
+                for h in range(HALVES):
+                    multiply_fp4(0, gate_sum[h][b], a, h, b, a == 0, a == PASSES - 1)
+            for b in range(BANKS):
+                for h in range(HALVES):
+                    multiply_fp4(1, hidden_sum[h][b], a, h, b, a == 0, False)
+
+        whd_raw = big.tile([P, PASSES, 4, N], F32, name="whd_raw", tag="big", align_bytes=64)
+        for a in range(PASSES):
+            nc.sync.dma_start(
+                whd_raw[:, a, :, :], whd[512 * a : 512 * (a + 1), :].rearrange("(p i) n -> p i n", i=4)
+            )
+        carried = []
+        for h in range(HALVES):
+            rows = big.tile([P, T], F32, name=f"carried{h}", tag="big", align_bytes=64)
+            nc.sync.dma_start(rows[:], rT[h * P : (h + 1) * P, :])
+            carried.append(rows)
+
+        carry_gate = keep.tile([P, HALVES, J], F32, name="carry_gate")
+        for h in range(HALVES):
+            for b in range(BANKS):
+                nc.scalar.activation(
+                    carry_gate[:, h, b * BANK : (b + 1) * BANK],
+                    gate_sum[h][b][:],
+                    ACT.Sigmoid,
+                    bias=neg_bias[:, h : h + 1],
+                    scale=-1.0,
+                )
+
+        whd_bf16 = keep.tile([P, PASSES, N, 4], BF16, name="whd_bf16", align_bytes=64)
+        whd_codes = keep.tile([P, PASSES, N], U32, name="whd_codes", align_bytes=64)
+        whd_scales = keep.tile([P, PASSES, N], U8, name="whd_scales", align_bytes=64)
+        for step in range(PASSES + 1):
+            if step < PASSES:
+                nc.vector.tensor_copy(
+                    whd_bf16[:, step, :, :], whd_raw[:, step, :, :].rearrange("p i n -> p n i")
+                )
+            if step > 0:
+                a = step - 1
+                nc.vector.quantize_mx(
+                    out=whd_codes[:, a, :].bitcast(FP8X4),
+                    scales=whd_scales[:, a, :],
+                    in_=whd_bf16[:, a, :, :].rearrange("p n i -> p (n i)"),
+                )
+
+        made = keep.tile([P, HALVES, J], F32, name="made")
+        for h in range(HALVES):
+            cols = slice(h * P, (h + 1) * P)
+            for b in range(BANKS):
+                for a in range(PASSES):
+                    multiply(
+                        hidden_sum[h][b],
+                        whd_codes[:, a, cols].bitcast(FP8X4),
+                        whd_scales[:, a, cols],
+                        a,
+                        b,
+                        False,
+                        a == PASSES - 1,
+                    )
+                nc.scalar.activation(made[:, h, b * BANK : (b + 1) * BANK], hidden_sum[h][b][:], ACT.Silu)
+
+        neg_gated = keep.tile([P, HALVES, J], F32, name="neg_gated")
+        kept = keep.tile([P, HALVES, J], F32, name="kept")
+        result = keep.tile([P, HALVES, J], F32, name="result")
+        for h in range(HALVES):
+            for b in range(BANKS):
+                cols = slice(b * BANK, (b + 1) * BANK)
+                nc.vector.scalar_tensor_tensor(
+                    neg_gated[:, h, cols], carry_gate[:, h, cols], 1.0, made[:, h, cols], ALU.subtract, ALU.mult
+                )
+        for h in range(HALVES):
+            cuts = EPILOGUE_CUTS[h]
+            for step in range(len(cuts)):
+                if step < len(cuts) - 1:
+                    j0, j1 = cuts[step], cuts[step + 1]
+                    nc.vector.tensor_tensor(
+                        kept[:, h, j0:j1], carried[h][:].indirect(listed(j0, j1)), carry_gate[:, h, j0:j1], ALU.mult
+                    )
+                if step > 0:
+                    j0, j1 = cuts[step - 1], cuts[step]
+                    nc.vector.tensor_tensor(
+                        result[:, h, j0:j1], kept[:, h, j0:j1], neg_gated[:, h, j0:j1], ALU.subtract
+                    )
+                    nc.sync.dma_start(out[h * P : (h + 1) * P, j0:j1], result[:, h, j0:j1])

@@ -22,11 +22,9 @@ HALVES = N // P
 BANK = 512
 BANKS = J // BANK
 GROUP = 16
-STAGE_ROW0 = 4
-STAGE_STEP = 8
-TAB_BYTES = PASSES * J
+SCALE_ROWS = ((2, 4), (66, 4), (5, 8))
 W_BYTES = PASSES * N
-PLANE_WORDS = (TAB_BYTES + 2 * W_BYTES) // 4
+STAGED_WORDS = (2 * W_BYTES + J) // 4
 EPILOGUE_CUTS = ((0, 512, 1024), (0, 256, 512, 768, 1024))
 
 
@@ -34,11 +32,9 @@ def tile_list_hwayt_dl_silu_kernel(
     tc, tab_words, tab_scales, wg_words, wg_scales, wh4_words, wh4_scales, whd, bg, rT, offs, out
 ):
     nc = tc.nc
-    staged_rows = slice(STAGE_ROW0, P, STAGE_STEP)
 
     with ExitStack() as ctx:
         keep = ctx.enter_context(tc.tile_pool(name="keep", bufs=1))
-        big = ctx.enter_context(tc.tile_pool(name="big", bufs=3))
         psum = ctx.enter_context(tc.psum_pool(name="psum", bufs=1))
 
         offsets = keep.tile([P, J // GROUP], U16, name="offsets")
@@ -47,57 +43,72 @@ def tile_list_hwayt_dl_silu_kernel(
         def listed(j0, j1):
             return offsets[:, j0 // GROUP : j1 // GROUP]
 
-        scale_window = keep.tile([P, PASSES, T // 4], I32, name="scale_window", tag="reused", align_bytes=64)
-        nc.vector.memset(scale_window[:], 0)
-        planes = keep.tile([P, PLANE_WORDS], I32, name="planes", align_bytes=64)
-        nc.vector.memset(planes[:], 0)
+        def block_rows(a, first, every):
+            start, step = SCALE_ROWS[a]
+            return slice(start + step * first, start + step * 15 + 1, step * every)
 
-        staged = keep.tile([P, PLANE_WORDS], I32, name="staged", align_bytes=64)
+        scale_window = keep.tile([P, T // 4], I32, name="scale_window", align_bytes=64)
+        scale_rows = tab_scales.rearrange("a q t -> (a q) t").bitcast(I32)
+        nc.sync.dma_start(
+            scale_window[0:P:2, :], scale_rows[0:32, :].unsqueeze(1).broadcast_to([32, 2, T // 4])
+        )
+        nc.sync.dma_start(
+            scale_window[1:P:2, :], scale_rows[32:48, :].unsqueeze(1).broadcast_to([16, 4, T // 4])
+        )
+        planes = []
+        for a in range(PASSES):
+            words = STAGED_WORDS if a == 0 else J // 4
+            plane = keep.tile([P, words], I32, name=f"plane{a}", align_bytes=64)
+            nc.vector.memset(plane[:], 0)
+            planes.append(plane)
+
+        staged = keep.tile([P, STAGED_WORDS], I32, name="staged", tag="area_b", align_bytes=64)
         for w, scales in enumerate((wg_scales, wh4_scales)):
-            c0 = (TAB_BYTES + w * W_BYTES) // 4
+            c0 = w * W_BYTES // 4
             nc.sync.dma_start(
-                staged[staged_rows, c0 : c0 + W_BYTES // 4].rearrange("q (a n) -> q a n", a=PASSES),
+                staged[block_rows(0, 0, 1), c0 : c0 + W_BYTES // 4].rearrange("q (a n) -> q a n", a=PASSES),
                 scales.rearrange("a q n -> q a n").bitcast(I32),
             )
-        nc.scalar.dma_start(
-            scale_window[staged_rows, :, :], tab_scales.rearrange("a q t -> q a t").bitcast(I32)
-        )
 
         bias = keep.tile([P, HALVES], F32, name="bias")
         with nc.allow_non_contiguous_dma(reason="one bias value for each partition"):
             nc.gpsimd.dma_start(bias[:], bg.rearrange("(h p) -> p h", p=P))
         neg_bias = keep.tile([P, HALVES], F32, name="neg_bias")
-        nc.gpsimd.tensor_scalar(neg_bias[:], bias[:], -1.0, 0.0, ALU.mult, ALU.add)
+        warm_up = keep.tile([P, HALVES], F32, name="warm_up")
+        nc.scalar.activation(warm_up[:], bias[:], ACT.Sigmoid)
+        nc.scalar.activation(neg_bias[:], bias[:], ACT.Copy, scale=-1.0)
 
-        def load_table(a):
-            words = big.tile([P, T], I32, name=f"table{a}", tag="big", align_bytes=64)
-            nc.sync.dma_start(words[:], tab_words[a].rearrange("p t i -> p (t i)").bitcast(I32))
-            return words
-
-        tables = [load_table(0)]
         fp4_words = []
         for name, words in (("wg", wg_words), ("wh4", wh4_words)):
             tile = keep.tile([P, PASSES, 2 * N], U8, name=name, align_bytes=64)
             nc.sync.dma_start(tile[:].bitcast(I32), words.rearrange("a p n -> p a n").bitcast(I32))
             fp4_words.append(tile)
-        tables += [load_table(a) for a in range(1, PASSES)]
 
-        picked_scales = keep.tile([P, PASSES, J], U8, name="picked_scales", align_bytes=64)
+        def load_table(a, words):
+            nc.sync.dma_start(words, tab_words[a].rearrange("p t i -> p (t i)").bitcast(I32))
+
+        first_table = keep.tile([P, T], I32, name="first_table", tag="area_c", align_bytes=64)
+        load_table(0, first_table[:])
+
+        picked_scales = keep.tile([P, J], U8, name="picked_scales", tag="area_a", align_bytes=64)
+        nc.vector.tensor_copy(picked_scales[:], scale_window[:].bitcast(U8).indirect(offsets[:]))
+        nc.vector.tensor_copy(staged[:, 2 * W_BYTES // 4 :], picked_scales[:].bitcast(I32))
+
+        later_tables = keep.tile([P, PASSES - 1, T], I32, name="later_tables", tag="area_a", align_bytes=64)
+        tables = [first_table[:]] + [later_tables[:, a - 1, :] for a in range(1, PASSES)]
         for a in range(PASSES):
-            nc.vector.tensor_copy(
-                picked_scales[:, a, :], scale_window[:, a, :].bitcast(U8).indirect(offsets[:])
-            )
-        nc.vector.tensor_copy(
-            staged[:, : TAB_BYTES // 4], picked_scales[:].rearrange("p a j -> p (a j)").bitcast(I32)
-        )
-        for r in range(4):
-            nc.scalar.dma_start(planes[r:P:32, :], staged[STAGE_ROW0 + STAGE_STEP * r : P : 32, :])
-        plane_bytes = planes[:].bitcast(U8)
+            if a > 0:
+                load_table(a, tables[a])
+            for r in range(4):
+                c0 = 0 if a == 0 else 2 * W_BYTES // 4
+                nc.sync.dma_start(planes[a][r:P:32, :], staged[block_rows(a, r, 4), c0:])
+        weight_planes = planes[0][:, : 2 * W_BYTES // 4].bitcast(U8)
+        table_planes = [planes[a][:, (2 * W_BYTES // 4 if a == 0 else 0) :].bitcast(U8) for a in range(PASSES)]
 
         gate_sum = [[psum.tile([P, BANK], F32, name=f"gate{h}{b}") for b in range(BANKS)] for h in range(HALVES)]
         hidden_sum = [[psum.tile([P, BANK], F32, name=f"hid{h}{b}") for b in range(BANKS)] for h in range(HALVES)]
 
-        picked = keep.tile([P, PASSES, J], U32, name="picked", tag="reused", align_bytes=64)
+        picked = keep.tile([P, PASSES, J], U32, name="picked", align_bytes=64)
 
         def multiply(acc, lhsT, lhsT_scale, a, b, start, stop):
             nc.tensor.matmul_mx(
@@ -105,21 +116,21 @@ def tile_list_hwayt_dl_silu_kernel(
                 lhsT=lhsT,
                 lhsT_scale=lhsT_scale,
                 rhs=picked[:, a, b * BANK : (b + 1) * BANK].bitcast(FP8X4),
-                rhs_scale=plane_bytes[:, a * J + b * BANK : a * J + (b + 1) * BANK],
+                rhs_scale=table_planes[a][:, b * BANK : (b + 1) * BANK],
                 start=start,
                 stop=stop,
             )
 
         def multiply_fp4(w, acc, a, h, b, start, stop):
-            c0 = TAB_BYTES + w * W_BYTES + a * N + h * P
+            c0 = w * W_BYTES + a * N + h * P
             codes = fp4_words[w][:, a, 2 * h * P : 2 * (h + 1) * P].bitcast(FP4X4)
-            multiply(acc, codes, plane_bytes[:, c0 : c0 + P], a, b, start, stop)
+            multiply(acc, codes, weight_planes[:, c0 : c0 + P], a, b, start, stop)
 
         for a in range(PASSES):
             for b in range(BANKS):
                 nc.vector.tensor_copy(
                     picked[:, a, b * BANK : (b + 1) * BANK],
-                    tables[a][:].bitcast(U32).indirect(listed(b * BANK, (b + 1) * BANK)),
+                    tables[a].bitcast(U32).indirect(listed(b * BANK, (b + 1) * BANK)),
                 )
             for b in range(BANKS):
                 for h in range(HALVES):
@@ -128,14 +139,14 @@ def tile_list_hwayt_dl_silu_kernel(
                 for h in range(HALVES):
                     multiply_fp4(1, hidden_sum[h][b], a, h, b, a == 0, False)
 
-        whd_raw = big.tile([P, PASSES, 4, N], F32, name="whd_raw", tag="big", align_bytes=64)
+        whd_raw = keep.tile([P, PASSES, 4, N], F32, name="whd_raw", tag="area_c", align_bytes=64)
         for a in range(PASSES):
             nc.sync.dma_start(
                 whd_raw[:, a, :, :], whd[512 * a : 512 * (a + 1), :].rearrange("(p i) n -> p i n", i=4)
             )
         carried = []
         for h in range(HALVES):
-            rows = big.tile([P, T], F32, name=f"carried{h}", tag="big", align_bytes=64)
+            rows = keep.tile([P, T], F32, name=f"carried{h}", tag=("area_b", "area_a")[h], align_bytes=64)
             nc.sync.dma_start(rows[:], rT[h * P : (h + 1) * P, :])
             carried.append(rows)
 
@@ -150,36 +161,38 @@ def tile_list_hwayt_dl_silu_kernel(
                     scale=-1.0,
                 )
 
-        whd_bf16 = keep.tile([P, PASSES, N, 4], BF16, name="whd_bf16", align_bytes=64)
-        whd_codes = keep.tile([P, PASSES, N], U32, name="whd_codes", align_bytes=64)
-        whd_scales = keep.tile([P, PASSES, N], U8, name="whd_scales", align_bytes=64)
-        for step in range(PASSES + 1):
-            if step < PASSES:
+        whd_bf16 = keep.tile([P, HALVES, PASSES, P, 4], BF16, name="whd_bf16", align_bytes=64)
+        whd_codes = keep.tile([P, HALVES, PASSES, P], U32, name="whd_codes", align_bytes=64)
+        whd_scales = keep.tile([P, HALVES, PASSES, P], U8, name="whd_scales", align_bytes=64)
+        pieces = [(h, a) for h in range(HALVES) for a in range(PASSES)]
+        for step in range(len(pieces) + 1):
+            if step < len(pieces):
+                h, a = pieces[step]
                 nc.vector.tensor_copy(
-                    whd_bf16[:, step, :, :], whd_raw[:, step, :, :].rearrange("p i n -> p n i")
+                    whd_bf16[:, h, a, :, :], whd_raw[:, a, :, h * P : (h + 1) * P].rearrange("p i n -> p n i")
                 )
             if step > 0:
-                a = step - 1
+                h, a = pieces[step - 1]
                 nc.vector.quantize_mx(
-                    out=whd_codes[:, a, :].bitcast(FP8X4),
-                    scales=whd_scales[:, a, :],
-                    in_=whd_bf16[:, a, :, :].rearrange("p n i -> p (n i)"),
+                    out=whd_codes[:, h, a, :].bitcast(FP8X4),
+                    scales=whd_scales[:, h, a, :],
+                    in_=whd_bf16[:, h, a, :, :].rearrange("p n i -> p (n i)"),
                 )
 
         made = keep.tile([P, HALVES, J], F32, name="made")
         for h in range(HALVES):
-            cols = slice(h * P, (h + 1) * P)
-            for b in range(BANKS):
-                for a in range(PASSES):
+            for a in range(PASSES):
+                for b in range(BANKS):
                     multiply(
                         hidden_sum[h][b],
-                        whd_codes[:, a, cols].bitcast(FP8X4),
-                        whd_scales[:, a, cols],
+                        whd_codes[:, h, a, :].bitcast(FP8X4),
+                        whd_scales[:, h, a, :],
                         a,
                         b,
                         False,
                         a == PASSES - 1,
                     )
+            for b in range(BANKS):
                 nc.scalar.activation(made[:, h, b * BANK : (b + 1) * BANK], hidden_sum[h][b][:], ACT.Silu)
 
         neg_gated = keep.tile([P, HALVES, J], F32, name="neg_gated")

@@ -22,10 +22,11 @@ HALVES = N // P
 BANK = 512
 BANKS = J // BANK
 GROUP = 16
-SCALE_ROWS = ((2, 4), (66, 4), (5, 8))
+SCALE_ROWS = ((32, 2), (33, 2), (96, 2))
 W_BYTES = PASSES * N
 STAGED_WORDS = (2 * W_BYTES + J) // 4
-EPILOGUE_CUTS = ((0, 512, 1024), (0, 256, 512, 768, 1024))
+AREA = 4 * T
+EPILOGUE_CUTS = ((0, 512, 1024), (0, 320, 640, 896, 1024))
 
 
 def tile_list_hwayt_dl_silu_kernel(
@@ -35,6 +36,7 @@ def tile_list_hwayt_dl_silu_kernel(
 
     with ExitStack() as ctx:
         keep = ctx.enter_context(tc.tile_pool(name="keep", bufs=1))
+        arena = ctx.enter_context(tc.tile_pool(name="arena", bufs=1))
         psum = ctx.enter_context(tc.psum_pool(name="psum", bufs=1))
 
         offsets = keep.tile([P, J // GROUP], U16, name="offsets")
@@ -48,13 +50,12 @@ def tile_list_hwayt_dl_silu_kernel(
             return slice(start + step * first, start + step * 15 + 1, step * every)
 
         scale_window = keep.tile([P, T // 4], I32, name="scale_window", align_bytes=64)
-        scale_rows = tab_scales.rearrange("a q t -> (a q) t").bitcast(I32)
+        nc.sync.dma_start(scale_window[32:64, :], tab_scales[0:2].rearrange("a q t -> q a t").bitcast(I32))
         nc.sync.dma_start(
-            scale_window[0:P:2, :], scale_rows[0:32, :].unsqueeze(1).broadcast_to([32, 2, T // 4])
+            scale_window[96:128, :], tab_scales[2].bitcast(I32).unsqueeze(1).broadcast_to([16, 2, T // 4])
         )
-        nc.sync.dma_start(
-            scale_window[1:P:2, :], scale_rows[32:48, :].unsqueeze(1).broadcast_to([16, 4, T // 4])
-        )
+        nc.vector.memset(scale_window[0:32, :], 0)
+        nc.vector.memset(scale_window[64:96, :], 0)
         planes = []
         for a in range(PASSES):
             words = STAGED_WORDS if a == 0 else J // 4
@@ -62,7 +63,7 @@ def tile_list_hwayt_dl_silu_kernel(
             nc.vector.memset(plane[:], 0)
             planes.append(plane)
 
-        staged = keep.tile([P, STAGED_WORDS], I32, name="staged", tag="area_b", align_bytes=64)
+        staged = keep.tile([P, STAGED_WORDS], I32, name="staged", align_bytes=64)
         for w, scales in enumerate((wg_scales, wh4_scales)):
             c0 = w * W_BYTES // 4
             nc.sync.dma_start(
@@ -75,8 +76,8 @@ def tile_list_hwayt_dl_silu_kernel(
             nc.gpsimd.dma_start(bias[:], bg.rearrange("(h p) -> p h", p=P))
         neg_bias = keep.tile([P, HALVES], F32, name="neg_bias")
         warm_up = keep.tile([P, HALVES], F32, name="warm_up")
-        nc.scalar.activation(warm_up[:], bias[:], ACT.Sigmoid)
-        nc.scalar.activation(neg_bias[:], bias[:], ACT.Copy, scale=-1.0)
+        nc.scalar.activation(warm_up[:], bias[:], ACT.Silu)
+        nc.scalar.activation(neg_bias[:], bias[:], ACT.Copy, scale=-0.5)
 
         fp4_words = []
         for name, words in (("wg", wg_words), ("wh4", wh4_words)):
@@ -84,21 +85,26 @@ def tile_list_hwayt_dl_silu_kernel(
             nc.sync.dma_start(tile[:].bitcast(I32), words.rearrange("a p n -> p a n").bitcast(I32))
             fp4_words.append(tile)
 
-        def load_table(a, words):
-            nc.sync.dma_start(words, tab_words[a].rearrange("p t i -> p (t i)").bitcast(I32))
+        def load_table(a):
+            words = arena.tile([P, T], I32, name=f"table{a}", offset=a * AREA, align_bytes=64)
+            nc.sync.dma_start(words[:], tab_words[a].rearrange("p t i -> p (t i)").bitcast(I32))
+            return words
 
-        first_table = keep.tile([P, T], I32, name="first_table", tag="area_c", align_bytes=64)
-        load_table(0, first_table[:])
+        def load_whd(a, pool, **place):
+            raw = pool.tile([P, 4, N], F32, name=f"whd_raw{a}", align_bytes=64, **place)
+            nc.sync.dma_start(raw[:], whd[512 * a : 512 * (a + 1), :].rearrange("(p i) n -> p i n", i=4))
+            return raw
 
-        picked_scales = keep.tile([P, J], U8, name="picked_scales", tag="area_a", align_bytes=64)
+        tables = [load_table(0)]
+        whd_raw = [load_whd(0, keep)]
+
+        picked_scales = arena.tile([P, J], U8, name="picked_scales", offset=2 * AREA - J // 2, align_bytes=64)
         nc.vector.tensor_copy(picked_scales[:], scale_window[:].bitcast(U8).indirect(offsets[:]))
         nc.vector.tensor_copy(staged[:, 2 * W_BYTES // 4 :], picked_scales[:].bitcast(I32))
 
-        later_tables = keep.tile([P, PASSES - 1, T], I32, name="later_tables", tag="area_a", align_bytes=64)
-        tables = [first_table[:]] + [later_tables[:, a - 1, :] for a in range(1, PASSES)]
         for a in range(PASSES):
             if a > 0:
-                load_table(a, tables[a])
+                tables.append(load_table(a))
             for r in range(4):
                 c0 = 0 if a == 0 else 2 * W_BYTES // 4
                 nc.sync.dma_start(planes[a][r:P:32, :], staged[block_rows(a, r, 4), c0:])
@@ -126,11 +132,35 @@ def tile_list_hwayt_dl_silu_kernel(
             codes = fp4_words[w][:, a, 2 * h * P : 2 * (h + 1) * P].bitcast(FP4X4)
             multiply(acc, codes, weight_planes[:, c0 : c0 + P], a, b, start, stop)
 
+        whd_bf16 = keep.tile([P, HALVES, PASSES, P, 4], BF16, name="whd_bf16", align_bytes=64)
+        whd_codes = keep.tile([P, HALVES, PASSES, P], U32, name="whd_codes", align_bytes=64)
+        whd_scales = keep.tile([P, HALVES, PASSES, P], U8, name="whd_scales", align_bytes=64)
+
+        def quantise_whd(pieces):
+            for step in range(len(pieces) + 1):
+                if step < len(pieces):
+                    h, a = pieces[step]
+                    nc.vector.tensor_copy(
+                        whd_bf16[:, h, a, :, :], whd_raw[a][:, :, h * P : (h + 1) * P].rearrange("p i n -> p n i")
+                    )
+                if step > 0:
+                    h, a = pieces[step - 1]
+                    nc.vector.quantize_mx(
+                        out=whd_codes[:, h, a, :].bitcast(FP8X4),
+                        scales=whd_scales[:, h, a, :],
+                        in_=whd_bf16[:, h, a, :, :].rearrange("p n i -> p (n i)"),
+                    )
+
+        def multiply_whd(a, h):
+            for b in range(BANKS):
+                codes = whd_codes[:, h, a, :].bitcast(FP8X4)
+                multiply(hidden_sum[h][b], codes, whd_scales[:, h, a, :], a, b, False, a == PASSES - 1)
+
         for a in range(PASSES):
             for b in range(BANKS):
                 nc.vector.tensor_copy(
                     picked[:, a, b * BANK : (b + 1) * BANK],
-                    tables[a].bitcast(U32).indirect(listed(b * BANK, (b + 1) * BANK)),
+                    tables[a][:].bitcast(U32).indirect(listed(b * BANK, (b + 1) * BANK)),
                 )
             for b in range(BANKS):
                 for h in range(HALVES):
@@ -138,62 +168,42 @@ def tile_list_hwayt_dl_silu_kernel(
             for b in range(BANKS):
                 for h in range(HALVES):
                     multiply_fp4(1, hidden_sum[h][b], a, h, b, a == 0, False)
+            if a == 0:
+                quantise_whd([(h, 0) for h in range(HALVES)])
+            if a == 1:
+                for h in range(HALVES):
+                    multiply_whd(0, h)
 
-        whd_raw = keep.tile([P, PASSES, 4, N], F32, name="whd_raw", tag="area_c", align_bytes=64)
-        for a in range(PASSES):
-            nc.sync.dma_start(
-                whd_raw[:, a, :, :], whd[512 * a : 512 * (a + 1), :].rearrange("(p i) n -> p i n", i=4)
-            )
+        whd_raw += [load_whd(a, arena, offset=(a - 1) * 16 * N) for a in range(1, PASSES)]
         carried = []
         for h in range(HALVES):
-            rows = keep.tile([P, T], F32, name=f"carried{h}", tag=("area_b", "area_a")[h], align_bytes=64)
+            rows = arena.tile([P, T], F32, name=f"carried{h}", offset=(h + 1) * AREA, align_bytes=64)
             nc.sync.dma_start(rows[:], rT[h * P : (h + 1) * P, :])
             carried.append(rows)
 
+        gate_tanh = keep.tile([P, HALVES, J], F32, name="gate_tanh")
         carry_gate = keep.tile([P, HALVES, J], F32, name="carry_gate")
-        for h in range(HALVES):
-            for b in range(BANKS):
+        for b in range(BANKS):
+            for h in range(HALVES):
                 nc.scalar.activation(
-                    carry_gate[:, h, b * BANK : (b + 1) * BANK],
+                    gate_tanh[:, h, b * BANK : (b + 1) * BANK],
                     gate_sum[h][b][:],
-                    ACT.Sigmoid,
+                    ACT.Tanh,
                     bias=neg_bias[:, h : h + 1],
-                    scale=-1.0,
+                    scale=-0.5,
                 )
 
-        whd_bf16 = keep.tile([P, HALVES, PASSES, P, 4], BF16, name="whd_bf16", align_bytes=64)
-        whd_codes = keep.tile([P, HALVES, PASSES, P], U32, name="whd_codes", align_bytes=64)
-        whd_scales = keep.tile([P, HALVES, PASSES, P], U8, name="whd_scales", align_bytes=64)
-        pieces = [(h, a) for h in range(HALVES) for a in range(PASSES)]
-        for step in range(len(pieces) + 1):
-            if step < len(pieces):
-                h, a = pieces[step]
-                nc.vector.tensor_copy(
-                    whd_bf16[:, h, a, :, :], whd_raw[:, a, :, h * P : (h + 1) * P].rearrange("p i n -> p n i")
-                )
-            if step > 0:
-                h, a = pieces[step - 1]
-                nc.vector.quantize_mx(
-                    out=whd_codes[:, h, a, :].bitcast(FP8X4),
-                    scales=whd_scales[:, h, a, :],
-                    in_=whd_bf16[:, h, a, :, :].rearrange("p n i -> p (n i)"),
-                )
+        quantise_whd([(h, a) for h in range(HALVES) for a in range(1, PASSES)])
 
         made = keep.tile([P, HALVES, J], F32, name="made")
         for h in range(HALVES):
-            for a in range(PASSES):
-                for b in range(BANKS):
-                    multiply(
-                        hidden_sum[h][b],
-                        whd_codes[:, h, a, :].bitcast(FP8X4),
-                        whd_scales[:, h, a, :],
-                        a,
-                        b,
-                        False,
-                        a == PASSES - 1,
-                    )
+            for a in range(1, PASSES):
+                multiply_whd(a, h)
             for b in range(BANKS):
                 nc.scalar.activation(made[:, h, b * BANK : (b + 1) * BANK], hidden_sum[h][b][:], ACT.Silu)
+            for b in range(BANKS):
+                cols = slice(b * BANK, (b + 1) * BANK)
+                nc.scalar.activation(carry_gate[:, h, cols], gate_tanh[:, h, cols], ACT.Copy, scale=0.5, bias=0.5)
 
         neg_gated = keep.tile([P, HALVES, J], F32, name="neg_gated")
         kept = keep.tile([P, HALVES, J], F32, name="kept")
@@ -202,7 +212,7 @@ def tile_list_hwayt_dl_silu_kernel(
             for b in range(BANKS):
                 cols = slice(b * BANK, (b + 1) * BANK)
                 nc.vector.scalar_tensor_tensor(
-                    neg_gated[:, h, cols], carry_gate[:, h, cols], 1.0, made[:, h, cols], ALU.subtract, ALU.mult
+                    neg_gated[:, h, cols], gate_tanh[:, h, cols], 1.0, made[:, h, cols], ALU.subtract, ALU.mult
                 )
         for h in range(HALVES):
             cuts = EPILOGUE_CUTS[h]
@@ -214,7 +224,7 @@ def tile_list_hwayt_dl_silu_kernel(
                     )
                 if step > 0:
                     j0, j1 = cuts[step - 1], cuts[step]
-                    nc.vector.tensor_tensor(
-                        result[:, h, j0:j1], kept[:, h, j0:j1], neg_gated[:, h, j0:j1], ALU.subtract
+                    nc.vector.scalar_tensor_tensor(
+                        result[:, h, j0:j1], neg_gated[:, h, j0:j1], -0.5, kept[:, h, j0:j1], ALU.mult, ALU.add
                     )
                     nc.sync.dma_start(out[h * P : (h + 1) * P, j0:j1], result[:, h, j0:j1])

@@ -90,17 +90,24 @@ def tile_list_hwayt_dl_silu_kernel(
             nc.sync.dma_start(words[:], tab_words[a].rearrange("p t i -> p (t i)").bitcast(I32))
             return words
 
-        def load_whd(a, pool, **place):
-            raw = pool.tile([P, 4, N], F32, name=f"whd_raw{a}", align_bytes=64, **place)
+        def load_whd(a):
+            raw = arena.tile([P, 4, N], F32, name=f"whd_raw{a}", offset=a * 16 * N, align_bytes=64)
             nc.sync.dma_start(raw[:], whd[512 * a : 512 * (a + 1), :].rearrange("(p i) n -> p i n", i=4))
             return raw
 
         tables = [load_table(0)]
-        whd_raw = [load_whd(0, keep)]
 
         picked_scales = arena.tile([P, J], U8, name="picked_scales", offset=2 * AREA - J // 2, align_bytes=64)
-        nc.vector.tensor_copy(picked_scales[:], scale_window[:].bitcast(U8).indirect(offsets[:]))
-        nc.vector.tensor_copy(staged[:, 2 * W_BYTES // 4 :], picked_scales[:].bitcast(I32))
+        for b in range(BANKS):
+            nc.vector.tensor_copy(
+                picked_scales[:, b * BANK : (b + 1) * BANK],
+                scale_window[:].bitcast(U8).indirect(listed(b * BANK, (b + 1) * BANK)),
+            )
+        for b in range(BANKS):
+            c0 = (2 * W_BYTES + b * BANK) // 4
+            nc.vector.tensor_copy(
+                staged[:, c0 : c0 + BANK // 4], picked_scales[:, b * BANK : (b + 1) * BANK].bitcast(I32)
+            )
 
         for a in range(PASSES):
             if a > 0:
@@ -168,13 +175,8 @@ def tile_list_hwayt_dl_silu_kernel(
             for b in range(BANKS):
                 for h in range(HALVES):
                     multiply_fp4(1, hidden_sum[h][b], a, h, b, a == 0, False)
-            if a == 0:
-                quantise_whd([(h, 0) for h in range(HALVES)])
-            if a == 1:
-                for h in range(HALVES):
-                    multiply_whd(0, h)
 
-        whd_raw += [load_whd(a, arena, offset=(a - 1) * 16 * N) for a in range(1, PASSES)]
+        whd_raw = [load_whd(a) for a in range(PASSES)]
         carried = []
         for h in range(HALVES):
             rows = arena.tile([P, T], F32, name=f"carried{h}", offset=(h + 1) * AREA, align_bytes=64)
@@ -193,11 +195,11 @@ def tile_list_hwayt_dl_silu_kernel(
                     scale=-0.5,
                 )
 
-        quantise_whd([(h, a) for h in range(HALVES) for a in range(1, PASSES)])
+        quantise_whd([(h, a) for h in range(HALVES) for a in range(PASSES)])
 
         made = keep.tile([P, HALVES, J], F32, name="made")
         for h in range(HALVES):
-            for a in range(1, PASSES):
+            for a in range(PASSES):
                 multiply_whd(a, h)
             for b in range(BANKS):
                 nc.scalar.activation(made[:, h, b * BANK : (b + 1) * BANK], hidden_sum[h][b][:], ACT.Silu)

@@ -22,7 +22,7 @@ HALVES = N // P
 BANK = 512
 BANKS = J // BANK
 GROUP = 16
-SCALE_ROWS = ((32, 2), (33, 2), (96, 2))
+SCALE_ROWS = ((32, 2), (33, 2), (112, 1))
 W_BYTES = PASSES * N
 STAGED_WORDS = (2 * W_BYTES + J) // 4
 AREA = 4 * T
@@ -51,11 +51,9 @@ def tile_list_hwayt_dl_silu_kernel(
 
         scale_window = keep.tile([P, T // 4], I32, name="scale_window", align_bytes=64)
         nc.sync.dma_start(scale_window[32:64, :], tab_scales[0:2].rearrange("a q t -> q a t").bitcast(I32))
-        nc.sync.dma_start(
-            scale_window[96:128, :], tab_scales[2].bitcast(I32).unsqueeze(1).broadcast_to([16, 2, T // 4])
-        )
+        nc.sync.dma_start(scale_window[112:128, :], tab_scales[2].bitcast(I32))
         nc.vector.memset(scale_window[0:32, :], 0)
-        nc.vector.memset(scale_window[64:96, :], 0)
+        nc.vector.memset(scale_window[64:112, :], 0)
         planes = []
         for a in range(PASSES):
             words = STAGED_WORDS if a == 0 else J // 4

@@ -69,19 +69,10 @@ def tile_list_hwayt_dl_silu_kernel(
                 scales.rearrange("a q n -> q a n").bitcast(I32),
             )
 
-        bias = keep.tile([P, HALVES], F32, name="bias")
-        with nc.allow_non_contiguous_dma(reason="one bias value for each partition"):
-            nc.gpsimd.dma_start(bias[:], bg.rearrange("(h p) -> p h", p=P))
-        neg_bias = keep.tile([P, HALVES], F32, name="neg_bias")
-        warm_up = keep.tile([P, HALVES], F32, name="warm_up")
-        nc.scalar.activation(warm_up[:], bias[:], ACT.Silu)
-        nc.scalar.activation(neg_bias[:], bias[:], ACT.Copy, scale=-0.5)
-
-        fp4_words = []
-        for name, words in (("wg", wg_words), ("wh4", wh4_words)):
-            tile = keep.tile([P, PASSES, 2 * N], U8, name=name, align_bytes=64)
-            nc.sync.dma_start(tile[:].bitcast(I32), words.rearrange("a p n -> p a n").bitcast(I32))
-            fp4_words.append(tile)
+        warm_in = keep.tile([P, 2], F32, name="warm_in")
+        warm_up = keep.tile([P, 2], F32, name="warm_up")
+        nc.gpsimd.memset(warm_in[:], 0.0)
+        nc.scalar.activation(warm_up[:], warm_in[:], ACT.Silu)
 
         def load_table(a):
             words = arena.tile([P, T], I32, name=f"table{a}", offset=a * AREA, align_bytes=64)
@@ -89,11 +80,19 @@ def tile_list_hwayt_dl_silu_kernel(
             return words
 
         def load_whd(a):
-            raw = arena.tile([P, 4, N], F32, name=f"whd_raw{a}", offset=a * 16 * N, align_bytes=64)
+            offset = 3 * AREA if a == 0 else a * 16 * N
+            raw = arena.tile([P, 4, N], F32, name=f"whd_raw{a}", offset=offset, align_bytes=64)
             nc.sync.dma_start(raw[:], whd[512 * a : 512 * (a + 1), :].rearrange("(p i) n -> p i n", i=4))
             return raw
 
         tables = [load_table(0)]
+
+        fp4_words = []
+        for name, words in (("wg", wg_words), ("wh4", wh4_words)):
+            tile = keep.tile([P, PASSES, 2 * N], U8, name=name, align_bytes=64)
+            nc.sync.dma_start(tile[:].bitcast(I32), words.rearrange("a p n -> p a n").bitcast(I32))
+            fp4_words.append(tile)
+        whd_raw = [load_whd(0)]
 
         picked_scales = arena.tile([P, J], U8, name="picked_scales", offset=2 * AREA - J // 2, align_bytes=64)
         for b in range(BANKS):
@@ -107,12 +106,12 @@ def tile_list_hwayt_dl_silu_kernel(
                 staged[:, c0 : c0 + BANK // 4], picked_scales[:, b * BANK : (b + 1) * BANK].bitcast(I32)
             )
 
-        for a in range(PASSES):
-            if a > 0:
-                tables.append(load_table(a))
-            for r in range(4):
-                c0 = 0 if a == 0 else 2 * W_BYTES // 4
-                nc.sync.dma_start(planes[a][r:P:32, :], staged[block_rows(a, r, 4), c0:])
+        for move in range(4 * PASSES):
+            a, r = divmod(move, 4)
+            c0 = 0 if a == 0 else 2 * W_BYTES // 4
+            nc.sync.dma_start(planes[a][r:P:32, :], staged[block_rows(a, r, 4), c0:])
+            if move % 6 == 5:
+                tables.append(load_table(len(tables)))
         weight_planes = planes[0][:, : 2 * W_BYTES // 4].bitcast(U8)
         table_planes = [planes[a][:, (2 * W_BYTES // 4 if a == 0 else 0) :].bitcast(U8) for a in range(PASSES)]
 
@@ -137,29 +136,27 @@ def tile_list_hwayt_dl_silu_kernel(
             codes = fp4_words[w][:, a, 2 * h * P : 2 * (h + 1) * P].bitcast(FP4X4)
             multiply(acc, codes, weight_planes[:, c0 : c0 + P], a, b, start, stop)
 
-        whd_bf16 = keep.tile([P, HALVES, PASSES, P, 4], BF16, name="whd_bf16", align_bytes=64)
-        whd_codes = keep.tile([P, HALVES, PASSES, P], U32, name="whd_codes", align_bytes=64)
-        whd_scales = keep.tile([P, HALVES, PASSES, P], U8, name="whd_scales", align_bytes=64)
+        whd_bf16 = [keep.tile([P, N, 4], BF16, name=f"whd_bf16{a}", align_bytes=64) for a in range(PASSES)]
+        whd_codes = keep.tile([P, PASSES, N], U32, name="whd_codes", align_bytes=64)
+        whd_scales = keep.tile([P, PASSES, N], U8, name="whd_scales", align_bytes=64)
 
-        def quantise_whd(pieces):
-            for step in range(len(pieces) + 1):
-                if step < len(pieces):
-                    h, a = pieces[step]
-                    nc.vector.tensor_copy(
-                        whd_bf16[:, h, a, :, :], whd_raw[a][:, :, h * P : (h + 1) * P].rearrange("p i n -> p n i")
-                    )
-                if step > 0:
-                    h, a = pieces[step - 1]
-                    nc.vector.quantize_mx(
-                        out=whd_codes[:, h, a, :].bitcast(FP8X4),
-                        scales=whd_scales[:, h, a, :],
-                        in_=whd_bf16[:, h, a, :, :].rearrange("p n i -> p (n i)"),
-                    )
+        def interleave_whd(copy, a, n0, n1):
+            copy(whd_bf16[a][:, n0:n1, :], whd_raw[a][:, :, n0:n1].rearrange("p i n -> p n i"))
+
+        def quantise_whd(a, n0, n1):
+            nc.vector.quantize_mx(
+                out=whd_codes[:, a, n0:n1].bitcast(FP8X4),
+                scales=whd_scales[:, a, n0:n1],
+                in_=whd_bf16[a][:, n0:n1, :].rearrange("p n i -> p (n i)"),
+            )
 
         def multiply_whd(a, h):
             for b in range(BANKS):
-                codes = whd_codes[:, h, a, :].bitcast(FP8X4)
-                multiply(hidden_sum[h][b], codes, whd_scales[:, h, a, :], a, b, False, a == PASSES - 1)
+                cols = slice(h * P, (h + 1) * P)
+                codes = whd_codes[:, a, cols].bitcast(FP8X4)
+                multiply(hidden_sum[h][b], codes, whd_scales[:, a, cols], a, b, False, a == PASSES - 1)
+
+        interleave_whd(nc.scalar.copy, 0, 0, N)
 
         for a in range(PASSES):
             for b in range(BANKS):
@@ -170,11 +167,19 @@ def tile_list_hwayt_dl_silu_kernel(
             for b in range(BANKS):
                 for h in range(HALVES):
                     multiply_fp4(0, gate_sum[h][b], a, h, b, a == 0, a == PASSES - 1)
-            for b in range(BANKS):
                 for h in range(HALVES):
                     multiply_fp4(1, hidden_sum[h][b], a, h, b, a == 0, False)
+            if a == 0:
+                quantise_whd(0, 0, N)
+                for h in range(HALVES):
+                    multiply_whd(0, h)
 
-        whd_raw = [load_whd(a) for a in range(PASSES)]
+        whd_raw.extend(load_whd(a) for a in range(1, PASSES))
+        bias = arena.tile([P, HALVES], F32, name="bias", offset=0, align_bytes=64)
+        with nc.allow_non_contiguous_dma(reason="one bias value for each partition"):
+            nc.sync.dma_start(bias[:], bg.rearrange("(h p) -> p h", p=P))
+        neg_bias = keep.tile([P, HALVES], F32, name="neg_bias")
+        nc.scalar.activation(neg_bias[:], bias[:], ACT.Copy, scale=-0.5)
         carried = []
         for h in range(HALVES):
             rows = arena.tile([P, T], F32, name=f"carried{h}", offset=(h + 1) * AREA, align_bytes=64)
@@ -193,11 +198,16 @@ def tile_list_hwayt_dl_silu_kernel(
                     scale=-0.5,
                 )
 
-        quantise_whd([(h, a) for h in range(HALVES) for a in range(PASSES)])
+        pieces = [(a, h * P, (h + 1) * P) for h in range(HALVES) for a in range(1, PASSES)]
+        for step in range(len(pieces) + 1):
+            if step < len(pieces):
+                interleave_whd(nc.vector.tensor_copy, *pieces[step])
+            if step > 0:
+                quantise_whd(*pieces[step - 1])
 
         made = keep.tile([P, HALVES, J], F32, name="made")
         for h in range(HALVES):
-            for a in range(PASSES):
+            for a in range(1, PASSES):
                 multiply_whd(a, h)
             for b in range(BANKS):
                 nc.scalar.activation(made[:, h, b * BANK : (b + 1) * BANK], hidden_sum[h][b][:], ACT.Silu)

@@ -1,6 +1,7 @@
 from contextlib import ExitStack
 
 import concourse.mybir as mybir
+from concourse.masks import make_identity
 
 K, N, T, J = 1536, 256, 4096, 1024
 FLOPS = 3 * 2 * K * N * J
@@ -26,7 +27,10 @@ SCALE_ROWS = ((32, 2), (33, 2), (112, 1))
 W_BYTES = PASSES * N
 STAGED_WORDS = (2 * W_BYTES + J) // 4
 AREA = 4 * T
-EPILOGUE_CUTS = ((0, 512, 1024), (0, 320, 640, 896, 1024))
+PIECE = 256
+TENSOR_CUTS = ((0, 512, 1024), ())
+ON_TENSOR = (J, 0)
+VECTOR_CUTS = (0, 320, 640, 896, 1024)
 
 
 def tile_list_hwayt_dl_silu_kernel(
@@ -69,10 +73,18 @@ def tile_list_hwayt_dl_silu_kernel(
                 scales.rearrange("a q n -> q a n").bitcast(I32),
             )
 
-        warm_in = keep.tile([P, 2], F32, name="warm_in")
+        identity = keep.tile([P, P], F32, name="identity")
+        make_identity(nc, identity[:])
         warm_up = keep.tile([P, 2], F32, name="warm_up")
-        nc.gpsimd.memset(warm_in[:], 0.0)
-        nc.scalar.activation(warm_up[:], warm_in[:], ACT.Silu)
+        nc.scalar.activation(warm_up[:], identity[:, 0:2], ACT.Silu)
+
+        bias_rows = keep.tile([P, P], F32, name="bias_rows")
+        nc.gpsimd.memset(bias_rows[:], 0.0)
+        nc.gpsimd.dma_start(bias_rows[0:HALVES, :], bg.rearrange("(h p) -> h p", p=P))
+        bias_turned = psum.tile([P, BANK], F32, name="bias_turned", tag="hid11")
+        nc.tensor.transpose(bias_turned[:, :P], bias_rows[:], identity[:])
+        half_bias = keep.tile([P, HALVES], F32, name="half_bias")
+        nc.scalar.activation(half_bias[:], bias_turned[:, :HALVES], ACT.Copy, scale=0.5)
 
         def load_table(a):
             words = arena.tile([P, T], I32, name=f"table{a}", offset=a * AREA, align_bytes=64)
@@ -115,8 +127,8 @@ def tile_list_hwayt_dl_silu_kernel(
         weight_planes = planes[0][:, : 2 * W_BYTES // 4].bitcast(U8)
         table_planes = [planes[a][:, (2 * W_BYTES // 4 if a == 0 else 0) :].bitcast(U8) for a in range(PASSES)]
 
-        gate_sum = [[psum.tile([P, BANK], F32, name=f"gate{h}{b}") for b in range(BANKS)] for h in range(HALVES)]
-        hidden_sum = [[psum.tile([P, BANK], F32, name=f"hid{h}{b}") for b in range(BANKS)] for h in range(HALVES)]
+        gate_sum = [[psum.tile([P, BANK], F32, name=f"gate{h}{b}", tag=f"gate{h}{b}") for b in range(BANKS)] for h in range(HALVES)]
+        hidden_sum = [[psum.tile([P, BANK], F32, name=f"hid{h}{b}", tag=f"hid{h}{b}") for b in range(BANKS)] for h in range(HALVES)]
 
         picked = keep.tile([P, PASSES, J], U32, name="picked", align_bytes=64)
 
@@ -141,7 +153,10 @@ def tile_list_hwayt_dl_silu_kernel(
         whd_scales = keep.tile([P, PASSES, N], U8, name="whd_scales", align_bytes=64)
 
         def interleave_whd(copy, a, n0, n1):
-            copy(whd_bf16[a][:, n0:n1, :], whd_raw[a][:, :, n0:n1].rearrange("p i n -> p n i"))
+            copy(
+                whd_bf16[a][:, n0:n1, :].rearrange("p (c n) i -> p c i n", n=4),
+                whd_raw[a][:, :, n0:n1].rearrange("p i (c n) -> p c i n", n=4),
+            )
 
         def quantise_whd(a, n0, n1):
             nc.vector.quantize_mx(
@@ -175,11 +190,6 @@ def tile_list_hwayt_dl_silu_kernel(
                     multiply_whd(0, h)
 
         whd_raw.extend(load_whd(a) for a in range(1, PASSES))
-        bias = arena.tile([P, HALVES], F32, name="bias", offset=0, align_bytes=64)
-        with nc.allow_non_contiguous_dma(reason="one bias value for each partition"):
-            nc.sync.dma_start(bias[:], bg.rearrange("(h p) -> p h", p=P))
-        neg_bias = keep.tile([P, HALVES], F32, name="neg_bias")
-        nc.scalar.activation(neg_bias[:], bias[:], ACT.Copy, scale=-0.5)
         carried = []
         for h in range(HALVES):
             rows = arena.tile([P, T], F32, name=f"carried{h}", offset=(h + 1) * AREA, align_bytes=64)
@@ -194,8 +204,8 @@ def tile_list_hwayt_dl_silu_kernel(
                     gate_tanh[:, h, b * BANK : (b + 1) * BANK],
                     gate_sum[h][b][:],
                     ACT.Tanh,
-                    bias=neg_bias[:, h : h + 1],
-                    scale=-0.5,
+                    bias=half_bias[:, h : h + 1],
+                    scale=0.5,
                 )
 
         pieces = [(a, h * P, (h + 1) * P) for h in range(HALVES) for a in range(1, PASSES)]
@@ -211,30 +221,70 @@ def tile_list_hwayt_dl_silu_kernel(
                 multiply_whd(a, h)
             for b in range(BANKS):
                 nc.scalar.activation(made[:, h, b * BANK : (b + 1) * BANK], hidden_sum[h][b][:], ACT.Silu)
-            for b in range(BANKS):
-                cols = slice(b * BANK, (b + 1) * BANK)
-                nc.scalar.activation(carry_gate[:, h, cols], gate_tanh[:, h, cols], ACT.Copy, scale=0.5, bias=0.5)
+            for j0, j1 in ((0, BANK), (BANK, J)):
+                cols = slice(j0, j1)
+                factor = 1.0 if j0 < ON_TENSOR[h] else 0.5
+                nc.scalar.activation(
+                    carry_gate[:, h, cols], gate_tanh[:, h, cols], ACT.Copy, scale=-factor, bias=factor
+                )
 
-        neg_gated = keep.tile([P, HALVES, J], F32, name="neg_gated")
+        gated = [
+            keep.tile([P, J], F32, name="gated0"),
+            arena.tile([P, J], F32, name="gated1", offset=AREA, align_bytes=64),
+        ]
         kept = keep.tile([P, HALVES, J], F32, name="kept")
+        turned = keep.tile([P, HALVES, J], F32, name="turned")
         result = keep.tile([P, HALVES, J], F32, name="result")
-        for h in range(HALVES):
+
+        def gate_made(h):
             for b in range(BANKS):
                 cols = slice(b * BANK, (b + 1) * BANK)
                 nc.vector.scalar_tensor_tensor(
-                    neg_gated[:, h, cols], gate_tanh[:, h, cols], 1.0, made[:, h, cols], ALU.subtract, ALU.mult
+                    gated[h][:, cols], gate_tanh[:, h, cols], 1.0, made[:, h, cols], ALU.add, ALU.mult
                 )
-        for h in range(HALVES):
-            cuts = EPILOGUE_CUTS[h]
-            for step in range(len(cuts)):
-                if step < len(cuts) - 1:
-                    j0, j1 = cuts[step], cuts[step + 1]
-                    nc.vector.tensor_tensor(
-                        kept[:, h, j0:j1], carried[h][:].indirect(listed(j0, j1)), carry_gate[:, h, j0:j1], ALU.mult
-                    )
-                if step > 0:
-                    j0, j1 = cuts[step - 1], cuts[step]
-                    nc.vector.scalar_tensor_tensor(
-                        result[:, h, j0:j1], neg_gated[:, h, j0:j1], -0.5, kept[:, h, j0:j1], ALU.mult, ALU.add
-                    )
-                    nc.sync.dma_start(out[h * P : (h + 1) * P, j0:j1], result[:, h, j0:j1])
+
+        gate_made(0)
+
+        def turn(bank, source, j0, j1, start, stop):
+            for j in range(j0, j1, P):
+                nc.tensor.matmul(
+                    bank[:, j - j0 : j - j0 + P],
+                    source[:, j : j + P],
+                    identity[:],
+                    start=start and j == j0,
+                    stop=stop and j == j1 - P,
+                    is_transpose=True,
+                )
+
+        pieces = [(h, j0, j1) for h in range(HALVES) for j0, j1 in zip(TENSOR_CUTS[h], TENSOR_CUTS[h][1:])]
+        sums = []
+        for (h, j0, j1), tag in zip(pieces, ("gate00", "gate01", "gate10")):
+            bank = psum.tile([P, BANK], F32, name=f"sum{h}{j0}", tag=tag)
+            turn(bank, gated[h], j0, j1, True, False)
+            sums.append(bank)
+
+        def keep_carried(h, j0, j1):
+            nc.vector.tensor_tensor(
+                kept[:, h, j0:j1], carried[h][:].indirect(listed(j0, j1)), carry_gate[:, h, j0:j1], ALU.mult
+            )
+
+        for (h, j0, j1), bank, tag in zip(pieces, sums, ("hid00", "hid01", "hid10")):
+            keep_carried(h, j0, j1)
+            turn(bank, kept[:, h, :], j0, j1, False, True)
+            nc.scalar.copy(turned[:, h, j0:j1], bank[:, : j1 - j0])
+            back = psum.tile([P, BANK], F32, name=f"back{h}{j0}", tag=tag)
+            turn(back, turned[:, h, :], j0, j1, True, True)
+            nc.scalar.activation(result[:, h, j0:j1], back[:, : j1 - j0], ACT.Copy, scale=0.5)
+            nc.scalar.dma_start(out[h * P : (h + 1) * P, j0:j1], result[:, h, j0:j1])
+
+        h = HALVES - 1
+        gate_made(h)
+        for step in range(len(VECTOR_CUTS)):
+            if step < len(VECTOR_CUTS) - 1:
+                keep_carried(h, VECTOR_CUTS[step], VECTOR_CUTS[step + 1])
+            if step > 0:
+                j0, j1 = VECTOR_CUTS[step - 1], VECTOR_CUTS[step]
+                nc.vector.scalar_tensor_tensor(
+                    result[:, h, j0:j1], gated[h][:, j0:j1], 0.5, kept[:, h, j0:j1], ALU.mult, ALU.add
+                )
+                nc.sync.dma_start(out[h * P : (h + 1) * P, j0:j1], result[:, h, j0:j1])

@@ -27,6 +27,7 @@ SCALE_ROWS = ((32, 2), (33, 2), (112, 1))
 W_BYTES = PASSES * N
 STAGED_WORDS = (2 * W_BYTES + J) // 4
 AREA = 4 * T
+GATES = 3 * AREA + 16 * N
 PIECE = 256
 TENSOR_CUTS = ((0, 512, 1024), ())
 ON_TENSOR = (J, 0)
@@ -97,13 +98,12 @@ def tile_list_hwayt_dl_silu_kernel(
             nc.sync.dma_start(raw[:], whd[512 * a : 512 * (a + 1), :].rearrange("(p i) n -> p i n", i=4))
             return raw
 
-        tables = [load_table(0)]
-
         fp4_words = []
         for name, words in (("wg", wg_words), ("wh4", wh4_words)):
             tile = keep.tile([P, PASSES, 2 * N], U8, name=name, align_bytes=64)
             nc.sync.dma_start(tile[:].bitcast(I32), words.rearrange("a p n -> p a n").bitcast(I32))
             fp4_words.append(tile)
+        tables = [load_table(0)]
         whd_raw = [load_whd(0)]
 
         picked_scales = arena.tile([P, J], U8, name="picked_scales", offset=2 * AREA - J // 2, align_bytes=64)
@@ -122,7 +122,7 @@ def tile_list_hwayt_dl_silu_kernel(
             a, r = divmod(move, 4)
             c0 = 0 if a == 0 else 2 * W_BYTES // 4
             nc.sync.dma_start(planes[a][r:P:32, :], staged[block_rows(a, r, 4), c0:])
-            if move % 6 == 5:
+            if move % 6 == 4:
                 tables.append(load_table(len(tables)))
         weight_planes = planes[0][:, : 2 * W_BYTES // 4].bitcast(U8)
         table_planes = [planes[a][:, (2 * W_BYTES // 4 if a == 0 else 0) :].bitcast(U8) for a in range(PASSES)]
@@ -148,30 +148,36 @@ def tile_list_hwayt_dl_silu_kernel(
             codes = fp4_words[w][:, a, 2 * h * P : 2 * (h + 1) * P].bitcast(FP4X4)
             multiply(acc, codes, weight_planes[:, c0 : c0 + P], a, b, start, stop)
 
-        whd_bf16 = [keep.tile([P, N, 4], BF16, name=f"whd_bf16{a}", align_bytes=64) for a in range(PASSES)]
-        whd_codes = keep.tile([P, PASSES, N], U32, name="whd_codes", align_bytes=64)
+        whd_bf16 = dict()
+        whd_codes = [
+            arena.tile([P, PASSES, P], U32, name=f"whd_codes{h}", offset=GATES + 4 * J * h, align_bytes=64)
+            for h in range(HALVES)
+        ]
         whd_scales = keep.tile([P, PASSES, N], U8, name="whd_scales", align_bytes=64)
 
-        def interleave_whd(copy, a, n0, n1):
+        def interleave_whd(copy, a, h, tag):
+            tile = keep.tile([P, P, 4], BF16, name=f"whd_bf16{a}{h}", tag=tag, align_bytes=64)
             copy(
-                whd_bf16[a][:, n0:n1, :].rearrange("p (c n) i -> p c i n", n=4),
-                whd_raw[a][:, :, n0:n1].rearrange("p i (c n) -> p c i n", n=4),
+                tile[:].rearrange("p (c n) i -> p c i n", n=4),
+                whd_raw[a][:, :, h * P : (h + 1) * P].rearrange("p i (c n) -> p c i n", n=4),
             )
+            whd_bf16.setdefault((a, h), tile)
 
-        def quantise_whd(a, n0, n1):
+        def quantise_whd(a, h):
             nc.vector.quantize_mx(
-                out=whd_codes[:, a, n0:n1].bitcast(FP8X4),
-                scales=whd_scales[:, a, n0:n1],
-                in_=whd_bf16[a][:, n0:n1, :].rearrange("p n i -> p (n i)"),
+                out=whd_codes[h][:, a, :].bitcast(FP8X4),
+                scales=whd_scales[:, a, h * P : (h + 1) * P],
+                in_=whd_bf16[a, h][:].rearrange("p n i -> p (n i)"),
             )
 
         def multiply_whd(a, h):
             for b in range(BANKS):
                 cols = slice(h * P, (h + 1) * P)
-                codes = whd_codes[:, a, cols].bitcast(FP8X4)
+                codes = whd_codes[h][:, a, :].bitcast(FP8X4)
                 multiply(hidden_sum[h][b], codes, whd_scales[:, a, cols], a, b, False, a == PASSES - 1)
 
-        interleave_whd(nc.scalar.copy, 0, 0, N)
+        for h in range(HALVES):
+            interleave_whd(nc.scalar.copy, 0, h, f"early{h}")
 
         for a in range(PASSES):
             for b in range(BANKS):
@@ -185,8 +191,8 @@ def tile_list_hwayt_dl_silu_kernel(
                 for h in range(HALVES):
                     multiply_fp4(1, hidden_sum[h][b], a, h, b, a == 0, False)
             if a == 0:
-                quantise_whd(0, 0, N)
                 for h in range(HALVES):
+                    quantise_whd(0, h)
                     multiply_whd(0, h)
 
         whd_raw.extend(load_whd(a) for a in range(1, PASSES))
@@ -197,35 +203,33 @@ def tile_list_hwayt_dl_silu_kernel(
             carried.append(rows)
 
         gate_tanh = keep.tile([P, HALVES, J], F32, name="gate_tanh")
-        carry_gate = keep.tile([P, HALVES, J], F32, name="carry_gate")
-        for b in range(BANKS):
-            for h in range(HALVES):
-                nc.scalar.activation(
-                    gate_tanh[:, h, b * BANK : (b + 1) * BANK],
-                    gate_sum[h][b][:],
-                    ACT.Tanh,
-                    bias=half_bias[:, h : h + 1],
-                    scale=0.5,
-                )
+        carry_gate = [
+            arena.tile([P, J], F32, name=f"carry_gate{h}", offset=GATES + 4 * J * h, align_bytes=64)
+            for h in range(HALVES)
+        ]
 
-        pieces = [(a, h * P, (h + 1) * P) for h in range(HALVES) for a in range(1, PASSES)]
-        for step in range(len(pieces) + 1):
-            if step < len(pieces):
-                interleave_whd(nc.vector.tensor_copy, *pieces[step])
-            if step > 0:
-                quantise_whd(*pieces[step - 1])
+        for h in range(HALVES):
+            for a in range(1, PASSES):
+                interleave_whd(nc.vector.tensor_copy, a, h, f"late{(a + h) % 2}")
+            for a in range(1, PASSES):
+                quantise_whd(a, h)
 
         made = keep.tile([P, HALVES, J], F32, name="made")
         for h in range(HALVES):
+            factor = 1.0 if ON_TENSOR[h] else 0.5
+            for b in range(BANKS):
+                cols = slice(b * BANK, (b + 1) * BANK)
+                nc.scalar.activation(
+                    gate_tanh[:, h, cols], gate_sum[h][b][:], ACT.Tanh, bias=half_bias[:, h : h + 1], scale=0.5
+                )
             for a in range(1, PASSES):
                 multiply_whd(a, h)
             for b in range(BANKS):
                 nc.scalar.activation(made[:, h, b * BANK : (b + 1) * BANK], hidden_sum[h][b][:], ACT.Silu)
-            for j0, j1 in ((0, BANK), (BANK, J)):
-                cols = slice(j0, j1)
-                factor = 1.0 if j0 < ON_TENSOR[h] else 0.5
+            for b in range(BANKS):
+                cols = slice(b * BANK, (b + 1) * BANK)
                 nc.scalar.activation(
-                    carry_gate[:, h, cols], gate_tanh[:, h, cols], ACT.Copy, scale=-factor, bias=factor
+                    carry_gate[h][:, cols], gate_tanh[:, h, cols], ACT.Copy, scale=-factor, bias=factor
                 )
 
         gated = [
@@ -265,7 +269,7 @@ def tile_list_hwayt_dl_silu_kernel(
 
         def keep_carried(h, j0, j1):
             nc.vector.tensor_tensor(
-                kept[:, h, j0:j1], carried[h][:].indirect(listed(j0, j1)), carry_gate[:, h, j0:j1], ALU.mult
+                kept[:, h, j0:j1], carried[h][:].indirect(listed(j0, j1)), carry_gate[h][:, j0:j1], ALU.mult
             )
 
         for (h, j0, j1), bank, tag in zip(pieces, sums, ("hid00", "hid01", "hid10")):

@@ -23,11 +23,10 @@ HALVES = N // P
 BANK = 512
 BANKS = J // BANK
 GROUP = 16
-SCALE_ROWS = ((32, 2), (33, 2), (112, 1))
 W_BYTES = PASSES * N
-STAGED_WORDS = (2 * W_BYTES + J) // 4
 AREA = 4 * T
 GATES = 3 * AREA + 16 * N
+SECOND_WINDOW = GATES + 8 * J
 PIECE = 256
 TENSOR_CUTS = ((0, 512, 1024), ())
 ON_TENSOR = (J, 0)
@@ -50,94 +49,94 @@ def tile_list_hwayt_dl_silu_kernel(
         def listed(j0, j1):
             return offsets[:, j0 // GROUP : j1 // GROUP]
 
-        def block_rows(a, first, every):
-            start, step = SCALE_ROWS[a]
-            return slice(start + step * first, start + step * 15 + 1, step * every)
-
-        scale_window = keep.tile([P, T // 4], I32, name="scale_window", align_bytes=64)
-        nc.sync.dma_start(scale_window[32:64, :], tab_scales[0:2].rearrange("a q t -> q a t").bitcast(I32))
-        nc.sync.dma_start(scale_window[112:128, :], tab_scales[2].bitcast(I32))
-        nc.vector.memset(scale_window[0:32, :], 0)
-        nc.vector.memset(scale_window[64:112, :], 0)
-        planes = []
-        for a in range(PASSES):
-            words = STAGED_WORDS if a == 0 else J // 4
-            plane = keep.tile([P, words], I32, name=f"plane{a}", align_bytes=64)
+        windows = [
+            keep.tile([P, T // 4], I32, name="window0", align_bytes=64),
+            arena.tile([P, T // 4], I32, name="window1", offset=SECOND_WINDOW, align_bytes=64),
+        ]
+        for window in windows:
+            nc.vector.memset(window[:], 0)
+        early_plane = keep.tile([P, (2 * W_BYTES + J) // 4], I32, name="early_plane", align_bytes=64)
+        late_plane = keep.tile([P, 2 * J // 4], I32, name="late_plane", align_bytes=64)
+        for plane in (early_plane, late_plane):
             nc.vector.memset(plane[:], 0)
-            planes.append(plane)
 
-        staged = keep.tile([P, STAGED_WORDS], I32, name="staged", align_bytes=64)
+        staged = keep.tile([P, (2 * W_BYTES + 2 * J) // 4], I32, name="staged", align_bytes=64)
         for w, scales in enumerate((wg_scales, wh4_scales)):
             c0 = w * W_BYTES // 4
             nc.sync.dma_start(
-                staged[block_rows(0, 0, 1), c0 : c0 + W_BYTES // 4].rearrange("q (a n) -> q a n", a=PASSES),
+                staged[32:96:4, c0 : c0 + W_BYTES // 4].rearrange("q (a n) -> q a n", a=PASSES),
                 scales.rearrange("a q n -> q a n").bitcast(I32),
             )
 
         identity = keep.tile([P, P], F32, name="identity")
-        make_identity(nc, identity[:])
+        nc.vector.memset(identity[:], 0.0)
+        make_identity(nc, identity[:], nomemset=True)
         warm_up = keep.tile([P, 2], F32, name="warm_up")
         nc.scalar.activation(warm_up[:], identity[:, 0:2], ACT.Silu)
 
-        bias_rows = keep.tile([P, P], F32, name="bias_rows")
-        nc.gpsimd.memset(bias_rows[:], 0.0)
-        nc.gpsimd.dma_start(bias_rows[0:HALVES, :], bg.rearrange("(h p) -> h p", p=P))
-        bias_turned = psum.tile([P, BANK], F32, name="bias_turned", tag="hid11")
-        nc.tensor.transpose(bias_turned[:, :P], bias_rows[:], identity[:])
-        half_bias = keep.tile([P, HALVES], F32, name="half_bias")
-        nc.scalar.activation(half_bias[:], bias_turned[:, :HALVES], ACT.Copy, scale=0.5)
 
         def load_table(a):
             words = arena.tile([P, T], I32, name=f"table{a}", offset=a * AREA, align_bytes=64)
             nc.sync.dma_start(words[:], tab_words[a].rearrange("p t i -> p (t i)").bitcast(I32))
             return words
 
-        def load_whd(a):
-            offset = 3 * AREA if a == 0 else a * 16 * N
-            raw = arena.tile([P, 4, N], F32, name=f"whd_raw{a}", offset=offset, align_bytes=64)
-            nc.sync.dma_start(raw[:], whd[512 * a : 512 * (a + 1), :].rearrange("(p i) n -> p i n", i=4))
-            return raw
+        def load_whd(a0, a1, offset):
+            raw = arena.tile([P, a1 - a0, 4, N], F32, name=f"whd_raw{a0}", offset=offset, align_bytes=64)
+            nc.sync.dma_start(raw[:], whd[512 * a0 : 512 * a1, :].rearrange("(a p i) n -> p a i n", p=P, i=4))
+            return [raw[:, a] for a in range(a1 - a0)]
 
         fp4_words = []
         for name, words in (("wg", wg_words), ("wh4", wh4_words)):
             tile = keep.tile([P, PASSES, 2 * N], U8, name=name, align_bytes=64)
             nc.sync.dma_start(tile[:].bitcast(I32), words.rearrange("a p n -> p a n").bitcast(I32))
             fp4_words.append(tile)
+        nc.sync.dma_start(windows[0][32:96:2, :], tab_scales[0:2].rearrange("a q t -> q a t").bitcast(I32))
+        nc.sync.dma_start(windows[1][34:96:4, :], tab_scales[2].bitcast(I32))
         tables = [load_table(0)]
-        whd_raw = [load_whd(0)]
+        whd_raw = load_whd(0, 1, 3 * AREA)
 
-        picked_scales = arena.tile([P, J], U8, name="picked_scales", offset=2 * AREA - J // 2, align_bytes=64)
-        for b in range(BANKS):
-            nc.vector.tensor_copy(
-                picked_scales[:, b * BANK : (b + 1) * BANK],
-                scale_window[:].bitcast(U8).indirect(listed(b * BANK, (b + 1) * BANK)),
-            )
-        for b in range(BANKS):
-            c0 = (2 * W_BYTES + b * BANK) // 4
-            nc.vector.tensor_copy(
-                staged[:, c0 : c0 + BANK // 4], picked_scales[:, b * BANK : (b + 1) * BANK].bitcast(I32)
-            )
+        bias_rows = keep.tile([P, P], F32, name="bias_rows")
+        nc.sync.dma_start(bias_rows[P - HALVES :, :], bg.rearrange("(h p) -> h p", p=P))
+        nc.vector.memset(bias_rows[: P - HALVES, :], 0.0)
+        bias_turned = psum.tile([P, BANK], F32, name="bias_turned", tag="hid11")
+        nc.tensor.transpose(bias_turned[:, :P], bias_rows[:], identity[:])
+        half_bias = keep.tile([P, HALVES], F32, name="half_bias")
+        nc.scalar.activation(half_bias[:], bias_turned[:, P - HALVES : P], ACT.Copy, scale=0.5)
 
-        for move in range(4 * PASSES):
-            a, r = divmod(move, 4)
-            c0 = 0 if a == 0 else 2 * W_BYTES // 4
-            nc.sync.dma_start(planes[a][r:P:32, :], staged[block_rows(a, r, 4), c0:])
-            if move % 6 == 4:
-                tables.append(load_table(len(tables)))
-        weight_planes = planes[0][:, : 2 * W_BYTES // 4].bitcast(U8)
-        table_planes = [planes[a][:, (2 * W_BYTES // 4 if a == 0 else 0) :].bitcast(U8) for a in range(PASSES)]
+        for g, (plane, row0, c_from) in enumerate(((early_plane, 32, 0), (late_plane, 34, 2 * W_BYTES // 4))):
+            picked_scales = arena.tile([P, J], U8, name=f"picked_scales{g}", offset=(g + 1) * AREA, align_bytes=64)
+            for b in range(BANKS):
+                nc.vector.tensor_copy(
+                    picked_scales[:, b * BANK : (b + 1) * BANK],
+                    windows[g][:].bitcast(U8).indirect(listed(b * BANK, (b + 1) * BANK)),
+                )
+            for b in range(BANKS):
+                c0 = (2 * W_BYTES + g * J + b * BANK) // 4
+                nc.vector.tensor_copy(
+                    staged[:, c0 : c0 + BANK // 4], picked_scales[:, b * BANK : (b + 1) * BANK].bitcast(I32)
+                )
+            for r in range(4):
+                nc.sync.dma_start(plane[r:P:32, :], staged[row0 + 4 * r : 96 : 16, c_from : c_from + plane.shape[1]])
+            tables.append(load_table(g + 1))
+        weight_planes = early_plane[:, : 2 * W_BYTES // 4].bitcast(U8)
+        table_planes = [
+            early_plane[:, 2 * W_BYTES // 4 :].bitcast(U8),
+            late_plane[:, : J // 4].bitcast(U8),
+            late_plane[:, J // 4 :].bitcast(U8),
+        ]
 
         gate_sum = [[psum.tile([P, BANK], F32, name=f"gate{h}{b}", tag=f"gate{h}{b}") for b in range(BANKS)] for h in range(HALVES)]
         hidden_sum = [[psum.tile([P, BANK], F32, name=f"hid{h}{b}", tag=f"hid{h}{b}") for b in range(BANKS)] for h in range(HALVES)]
 
-        picked = keep.tile([P, PASSES, J], U32, name="picked", align_bytes=64)
+        picked = [arena.tile([P, J], U32, name="picked0", offset=SECOND_WINDOW, align_bytes=64)]
+        picked.extend(keep.tile([P, J], U32, name=f"picked{a}", align_bytes=64) for a in range(1, PASSES))
 
         def multiply(acc, lhsT, lhsT_scale, a, b, start, stop):
             nc.tensor.matmul_mx(
                 out=acc[:],
                 lhsT=lhsT,
                 lhsT_scale=lhsT_scale,
-                rhs=picked[:, a, b * BANK : (b + 1) * BANK].bitcast(FP8X4),
+                rhs=picked[a][:, b * BANK : (b + 1) * BANK].bitcast(FP8X4),
                 rhs_scale=table_planes[a][:, b * BANK : (b + 1) * BANK],
                 start=start,
                 stop=stop,
@@ -182,7 +181,7 @@ def tile_list_hwayt_dl_silu_kernel(
         for a in range(PASSES):
             for b in range(BANKS):
                 nc.vector.tensor_copy(
-                    picked[:, a, b * BANK : (b + 1) * BANK],
+                    picked[a][:, b * BANK : (b + 1) * BANK],
                     tables[a][:].bitcast(U32).indirect(listed(b * BANK, (b + 1) * BANK)),
                 )
             for b in range(BANKS):
@@ -193,9 +192,11 @@ def tile_list_hwayt_dl_silu_kernel(
             if a == 0:
                 for h in range(HALVES):
                     quantise_whd(0, h)
+            if a == 1:
+                for h in range(HALVES):
                     multiply_whd(0, h)
 
-        whd_raw.extend(load_whd(a) for a in range(1, PASSES))
+        whd_raw.extend(load_whd(1, PASSES, 0))
         carried = []
         for h in range(HALVES):
             rows = arena.tile([P, T], F32, name=f"carried{h}", offset=(h + 1) * AREA, align_bytes=64)

@@ -169,11 +169,10 @@ def tile_list_hwayt_dl_silu_kernel(
                 in_=whd_bf16[a, h][:].rearrange("p n i -> p (n i)"),
             )
 
-        def multiply_whd(a, h):
-            for b in range(BANKS):
-                cols = slice(h * P, (h + 1) * P)
-                codes = whd_codes[h][:, a, :].bitcast(FP8X4)
-                multiply(hidden_sum[h][b], codes, whd_scales[:, a, cols], a, b, False, a == PASSES - 1)
+        def multiply_whd(a, h, b, stop):
+            cols = slice(h * P, (h + 1) * P)
+            codes = whd_codes[h][:, a, :].bitcast(FP8X4)
+            multiply(hidden_sum[h][b], codes, whd_scales[:, a, cols], a, b, False, stop)
 
         for h in range(HALVES):
             interleave_whd(nc.scalar.copy, 0, h, f"early{h}")
@@ -187,14 +186,15 @@ def tile_list_hwayt_dl_silu_kernel(
             for b in range(BANKS):
                 for h in range(HALVES):
                     multiply_fp4(0, gate_sum[h][b], a, h, b, a == 0, a == PASSES - 1)
-                for h in range(HALVES):
+                for h in range(HALVES if a < PASSES - 1 else 1):
                     multiply_fp4(1, hidden_sum[h][b], a, h, b, a == 0, False)
             if a == 0:
                 for h in range(HALVES):
                     quantise_whd(0, h)
             if a == 1:
                 for h in range(HALVES):
-                    multiply_whd(0, h)
+                    for b in range(BANKS):
+                        multiply_whd(0, h, b, False)
 
         whd_raw.extend(load_whd(1, PASSES, 0))
         carried = []
@@ -223,8 +223,11 @@ def tile_list_hwayt_dl_silu_kernel(
                 nc.scalar.activation(
                     gate_tanh[:, h, cols], gate_sum[h][b][:], ACT.Tanh, bias=half_bias[:, h : h + 1], scale=0.5
                 )
-            for a in range(1, PASSES):
-                multiply_whd(a, h)
+            for b in range(BANKS):
+                for a in range(1, PASSES):
+                    multiply_whd(a, h, b, h == 0 and a == PASSES - 1)
+                if h == 1:
+                    multiply_fp4(1, hidden_sum[h][b], PASSES - 1, h, b, False, True)
             for b in range(BANKS):
                 nc.scalar.activation(made[:, h, b * BANK : (b + 1) * BANK], hidden_sum[h][b][:], ACT.Silu)
             for b in range(BANKS):
@@ -263,7 +266,7 @@ def tile_list_hwayt_dl_silu_kernel(
 
         pieces = [(h, j0, j1) for h in range(HALVES) for j0, j1 in zip(TENSOR_CUTS[h], TENSOR_CUTS[h][1:])]
         sums = []
-        for (h, j0, j1), tag in zip(pieces, ("gate00", "gate01", "gate10")):
+        for (h, j0, j1), tag in zip(pieces, ("hid10", "hid11")):
             bank = psum.tile([P, BANK], F32, name=f"sum{h}{j0}", tag=tag)
             turn(bank, gated[h], j0, j1, True, False)
             sums.append(bank)
@@ -273,14 +276,14 @@ def tile_list_hwayt_dl_silu_kernel(
                 kept[:, h, j0:j1], carried[h][:].indirect(listed(j0, j1)), carry_gate[h][:, j0:j1], ALU.mult
             )
 
-        for (h, j0, j1), bank, tag in zip(pieces, sums, ("hid00", "hid01", "hid10")):
+        for (h, j0, j1), bank, tag in zip(pieces, sums, ("hid00", "hid01")):
             keep_carried(h, j0, j1)
             turn(bank, kept[:, h, :], j0, j1, False, True)
             nc.scalar.copy(turned[:, h, j0:j1], bank[:, : j1 - j0])
             back = psum.tile([P, BANK], F32, name=f"back{h}{j0}", tag=tag)
             turn(back, turned[:, h, :], j0, j1, True, True)
             nc.scalar.activation(result[:, h, j0:j1], back[:, : j1 - j0], ACT.Copy, scale=0.5)
-            nc.scalar.dma_start(out[h * P : (h + 1) * P, j0:j1], result[:, h, j0:j1])
+            nc.sync.dma_start(out[h * P : (h + 1) * P, j0:j1], result[:, h, j0:j1])
 
         h = HALVES - 1
         gate_made(h)

@@ -91,8 +91,8 @@ def tile_list_hwayt_dl_silu_kernel(
             nc.sync.dma_start(tile[:].bitcast(I32), words.rearrange("a p n -> p a n").bitcast(I32))
             fp4_words.append(tile)
         nc.sync.dma_start(windows[0][32:96:2, :], tab_scales[0:2].rearrange("a q t -> q a t").bitcast(I32))
-        nc.sync.dma_start(windows[1][34:96:4, :], tab_scales[2].bitcast(I32))
         tables = [load_table(0)]
+        nc.sync.dma_start(windows[1][34:96:4, :], tab_scales[2].bitcast(I32))
         whd_raw = load_whd(0, 1, 3 * AREA)
 
         bias_rows = keep.tile([P, P], F32, name="bias_rows")
@@ -276,14 +276,14 @@ def tile_list_hwayt_dl_silu_kernel(
                 kept[:, h, j0:j1], carried[h][:].indirect(listed(j0, j1)), carry_gate[h][:, j0:j1], ALU.mult
             )
 
-        for (h, j0, j1), bank, tag in zip(pieces, sums, ("hid00", "hid01")):
+        for (h, j0, j1), bank, tag, queue in zip(pieces, sums, ("hid00", "hid01"), (nc.sync, nc.scalar)):
             keep_carried(h, j0, j1)
             turn(bank, kept[:, h, :], j0, j1, False, True)
             nc.scalar.copy(turned[:, h, j0:j1], bank[:, : j1 - j0])
             back = psum.tile([P, BANK], F32, name=f"back{h}{j0}", tag=tag)
             turn(back, turned[:, h, :], j0, j1, True, True)
             nc.scalar.activation(result[:, h, j0:j1], back[:, : j1 - j0], ACT.Copy, scale=0.5)
-            nc.sync.dma_start(out[h * P : (h + 1) * P, j0:j1], result[:, h, j0:j1])
+            queue.dma_start(out[h * P : (h + 1) * P, j0:j1], result[:, h, j0:j1])
 
         h = HALVES - 1
         gate_made(h)

@@ -90,13 +90,13 @@ def tile_list_hwayt_dl_silu_kernel(
             tile = keep.tile([P, PASSES, 2 * N], U8, name=name, align_bytes=64)
             nc.sync.dma_start(tile[:].bitcast(I32), words.rearrange("a p n -> p a n").bitcast(I32))
             fp4_words.append(tile)
+        bias_rows = keep.tile([P, P], F32, name="bias_rows")
+        nc.sync.dma_start(bias_rows[P - HALVES :, :], bg.rearrange("(h p) -> h p", p=P))
         nc.sync.dma_start(windows[0][32:96:2, :], tab_scales[0:2].rearrange("a q t -> q a t").bitcast(I32))
         tables = [load_table(0)]
         nc.sync.dma_start(windows[1][34:96:4, :], tab_scales[2].bitcast(I32))
         whd_raw = load_whd(0, 1, 3 * AREA)
 
-        bias_rows = keep.tile([P, P], F32, name="bias_rows")
-        nc.sync.dma_start(bias_rows[P - HALVES :, :], bg.rearrange("(h p) -> h p", p=P))
         nc.vector.memset(bias_rows[: P - HALVES, :], 0.0)
         bias_turned = psum.tile([P, BANK], F32, name="bias_turned", tag="hid11")
         nc.tensor.transpose(bias_turned[:, :P], bias_rows[:], identity[:])

@@ -43,6 +43,12 @@ def tile_list_hwayt_dl_silu_kernel(
         arena = ctx.enter_context(tc.tile_pool(name="arena", bufs=1))
         psum = ctx.enter_context(tc.psum_pool(name="psum", bufs=1))
 
+        fp4_words = []
+        for name, words in (("wg", wg_words), ("wh4", wh4_words)):
+            tile = keep.tile([P, PASSES, 2 * N], U8, name=name, align_bytes=64)
+            nc.sync.dma_start(tile[:].bitcast(I32), words.rearrange("a p n -> p a n").bitcast(I32))
+            fp4_words.append(tile)
+
         offsets = keep.tile([P, J // GROUP], U16, name="offsets")
         nc.sync.dma_start(offsets[:], offs)
 
@@ -85,11 +91,6 @@ def tile_list_hwayt_dl_silu_kernel(
             nc.sync.dma_start(raw[:], whd[512 * a0 : 512 * a1, :].rearrange("(a p i) n -> p a i n", p=P, i=4))
             return [raw[:, a] for a in range(a1 - a0)]
 
-        fp4_words = []
-        for name, words in (("wg", wg_words), ("wh4", wh4_words)):
-            tile = keep.tile([P, PASSES, 2 * N], U8, name=name, align_bytes=64)
-            nc.sync.dma_start(tile[:].bitcast(I32), words.rearrange("a p n -> p a n").bitcast(I32))
-            fp4_words.append(tile)
         bias_rows = keep.tile([P, P], F32, name="bias_rows")
         nc.sync.dma_start(bias_rows[P - HALVES :, :], bg.rearrange("(h p) -> h p", p=P))
         nc.sync.dma_start(windows[0][32:96:2, :], tab_scales[0:2].rearrange("a q t -> q a t").bitcast(I32))

@@ -24,13 +24,13 @@ BANK = 512
 BANKS = J // BANK
 GROUP = 16
 W_BYTES = PASSES * N
+
 AREA = 4 * T
-GATES = 3 * AREA + 16 * N
-SECOND_WINDOW = GATES + 8 * J
-PIECE = 256
-TENSOR_CUTS = ((0, 512, 1024), ())
-ON_TENSOR = (J, 0)
-VECTOR_CUTS = (0, 320, 640, 896, 1024)
+FIRST_WHD = 3 * AREA
+GATES = FIRST_WHD + 4 * 4 * N
+SECOND_WINDOW = GATES + HALVES * 4 * J
+
+LAST_CUTS = (0, 320, 640, 896, 1024)
 
 
 def tile_list_hwayt_dl_silu_kernel(
@@ -61,10 +61,10 @@ def tile_list_hwayt_dl_silu_kernel(
         ]
         for window in windows:
             nc.vector.memset(window[:], 0)
-        early_plane = keep.tile([P, (2 * W_BYTES + J) // 4], I32, name="early_plane", align_bytes=64)
-        late_plane = keep.tile([P, 2 * J // 4], I32, name="late_plane", align_bytes=64)
-        for plane in (early_plane, late_plane):
-            nc.vector.memset(plane[:], 0)
+        early_planes = keep.tile([P, (2 * W_BYTES + J) // 4], I32, name="early_plane", align_bytes=64)
+        late_planes = keep.tile([P, 2 * J // 4], I32, name="late_plane", align_bytes=64)
+        for planes in (early_planes, late_planes):
+            nc.vector.memset(planes[:], 0)
 
         staged = keep.tile([P, (2 * W_BYTES + 2 * J) // 4], I32, name="staged", align_bytes=64)
         for w, scales in enumerate((wg_scales, wh4_scales)):
@@ -79,7 +79,6 @@ def tile_list_hwayt_dl_silu_kernel(
         make_identity(nc, identity[:], nomemset=True)
         warm_up = keep.tile([P, 2], F32, name="warm_up")
         nc.scalar.activation(warm_up[:], identity[:, 0:2], ACT.Silu)
-
 
         def load_table(a):
             words = arena.tile([P, T], I32, name=f"table{a}", offset=a * AREA, align_bytes=64)
@@ -96,7 +95,7 @@ def tile_list_hwayt_dl_silu_kernel(
         nc.sync.dma_start(windows[0][32:96:2, :], tab_scales[0:2].rearrange("a q t -> q a t").bitcast(I32))
         tables = [load_table(0)]
         nc.sync.dma_start(windows[1][34:96:4, :], tab_scales[2].bitcast(I32))
-        whd_raw = load_whd(0, 1, 3 * AREA)
+        whd_raw = load_whd(0, 1, FIRST_WHD)
 
         nc.vector.memset(bias_rows[: P - HALVES, :], 0.0)
         bias_turned = psum.tile([P, BANK], F32, name="bias_turned", tag="hid11")
@@ -104,7 +103,7 @@ def tile_list_hwayt_dl_silu_kernel(
         half_bias = keep.tile([P, HALVES], F32, name="half_bias")
         nc.scalar.activation(half_bias[:], bias_turned[:, P - HALVES : P], ACT.Copy, scale=0.5)
 
-        for g, (plane, row0, c_from) in enumerate(((early_plane, 32, 0), (late_plane, 34, 2 * W_BYTES // 4))):
+        for g, (planes, row0, first_word) in enumerate(((early_planes, 32, 0), (late_planes, 34, 2 * W_BYTES // 4))):
             picked_scales = arena.tile([P, J], U8, name=f"picked_scales{g}", offset=(g + 1) * AREA, align_bytes=64)
             for b in range(BANKS):
                 nc.vector.tensor_copy(
@@ -117,27 +116,35 @@ def tile_list_hwayt_dl_silu_kernel(
                     staged[:, c0 : c0 + BANK // 4], picked_scales[:, b * BANK : (b + 1) * BANK].bitcast(I32)
                 )
             for r in range(4):
-                nc.sync.dma_start(plane[r:P:32, :], staged[row0 + 4 * r : 96 : 16, c_from : c_from + plane.shape[1]])
+                nc.sync.dma_start(
+                    planes[r:P:32, :], staged[row0 + 4 * r : 96 : 16, first_word : first_word + planes.shape[1]]
+                )
             tables.append(load_table(g + 1))
-        weight_planes = early_plane[:, : 2 * W_BYTES // 4].bitcast(U8)
+        weight_planes = early_planes[:, : 2 * W_BYTES // 4].bitcast(U8)
         table_planes = [
-            early_plane[:, 2 * W_BYTES // 4 :].bitcast(U8),
-            late_plane[:, : J // 4].bitcast(U8),
-            late_plane[:, J // 4 :].bitcast(U8),
+            early_planes[:, 2 * W_BYTES // 4 :].bitcast(U8),
+            late_planes[:, : J // 4].bitcast(U8),
+            late_planes[:, J // 4 :].bitcast(U8),
         ]
 
-        gate_sum = [[psum.tile([P, BANK], F32, name=f"gate{h}{b}", tag=f"gate{h}{b}") for b in range(BANKS)] for h in range(HALVES)]
-        hidden_sum = [[psum.tile([P, BANK], F32, name=f"hid{h}{b}", tag=f"hid{h}{b}") for b in range(BANKS)] for h in range(HALVES)]
+        gate_sum = [
+            [psum.tile([P, BANK], F32, name=f"gate{h}{b}", tag=f"gate{h}{b}") for b in range(BANKS)]
+            for h in range(HALVES)
+        ]
+        hidden_sum = [
+            [psum.tile([P, BANK], F32, name=f"hid{h}{b}", tag=f"hid{h}{b}") for b in range(BANKS)]
+            for h in range(HALVES)
+        ]
 
-        picked = [arena.tile([P, J], U32, name="picked0", offset=SECOND_WINDOW, align_bytes=64)]
-        picked.extend(keep.tile([P, J], U32, name=f"picked{a}", align_bytes=64) for a in range(1, PASSES))
+        picked_words = [arena.tile([P, J], U32, name="picked0", offset=SECOND_WINDOW, align_bytes=64)]
+        picked_words.extend(keep.tile([P, J], U32, name=f"picked{a}", align_bytes=64) for a in range(1, PASSES))
 
         def multiply(acc, lhsT, lhsT_scale, a, b, start, stop):
             nc.tensor.matmul_mx(
                 out=acc[:],
                 lhsT=lhsT,
                 lhsT_scale=lhsT_scale,
-                rhs=picked[a][:, b * BANK : (b + 1) * BANK].bitcast(FP8X4),
+                rhs=picked_words[a][:, b * BANK : (b + 1) * BANK].bitcast(FP8X4),
                 rhs_scale=table_planes[a][:, b * BANK : (b + 1) * BANK],
                 start=start,
                 stop=stop,
@@ -171,28 +178,28 @@ def tile_list_hwayt_dl_silu_kernel(
             )
 
         def multiply_whd(a, h, b, stop):
-            cols = slice(h * P, (h + 1) * P)
             codes = whd_codes[h][:, a, :].bitcast(FP8X4)
-            multiply(hidden_sum[h][b], codes, whd_scales[:, a, cols], a, b, False, stop)
+            multiply(hidden_sum[h][b], codes, whd_scales[:, a, h * P : (h + 1) * P], a, b, False, stop)
 
         for h in range(HALVES):
             interleave_whd(nc.scalar.copy, 0, h, f"early{h}")
 
+        last_pass = PASSES - 1
         for a in range(PASSES):
             for b in range(BANKS):
                 nc.vector.tensor_copy(
-                    picked[a][:, b * BANK : (b + 1) * BANK],
+                    picked_words[a][:, b * BANK : (b + 1) * BANK],
                     tables[a][:].bitcast(U32).indirect(listed(b * BANK, (b + 1) * BANK)),
                 )
             for b in range(BANKS):
                 for h in range(HALVES):
-                    multiply_fp4(0, gate_sum[h][b], a, h, b, a == 0, a == PASSES - 1)
-                for h in range(HALVES if a < PASSES - 1 else 1):
+                    multiply_fp4(0, gate_sum[h][b], a, h, b, a == 0, a == last_pass)
+                for h in range(HALVES if a < last_pass else 1):
                     multiply_fp4(1, hidden_sum[h][b], a, h, b, a == 0, False)
             if a == 0:
                 for h in range(HALVES):
                     quantise_whd(0, h)
-            if a == 1:
+            if a == last_pass - 1:
                 for h in range(HALVES):
                     for b in range(BANKS):
                         multiply_whd(0, h, b, False)
@@ -217,8 +224,7 @@ def tile_list_hwayt_dl_silu_kernel(
                 quantise_whd(a, h)
 
         made = keep.tile([P, HALVES, J], F32, name="made")
-        for h in range(HALVES):
-            factor = 1.0 if ON_TENSOR[h] else 0.5
+        for h, factor in enumerate((1.0, 0.5)):
             for b in range(BANKS):
                 cols = slice(b * BANK, (b + 1) * BANK)
                 nc.scalar.activation(
@@ -226,9 +232,9 @@ def tile_list_hwayt_dl_silu_kernel(
                 )
             for b in range(BANKS):
                 for a in range(1, PASSES):
-                    multiply_whd(a, h, b, h == 0 and a == PASSES - 1)
+                    multiply_whd(a, h, b, h == 0 and a == last_pass)
                 if h == 1:
-                    multiply_fp4(1, hidden_sum[h][b], PASSES - 1, h, b, False, True)
+                    multiply_fp4(1, hidden_sum[h][b], last_pass, h, b, False, True)
             for b in range(BANKS):
                 nc.scalar.activation(made[:, h, b * BANK : (b + 1) * BANK], hidden_sum[h][b][:], ACT.Silu)
             for b in range(BANKS):
@@ -242,7 +248,7 @@ def tile_list_hwayt_dl_silu_kernel(
             arena.tile([P, J], F32, name="gated1", offset=AREA, align_bytes=64),
         ]
         kept = keep.tile([P, HALVES, J], F32, name="kept")
-        turned = keep.tile([P, HALVES, J], F32, name="turned")
+        turned = keep.tile([P, J], F32, name="turned")
         result = keep.tile([P, HALVES, J], F32, name="result")
 
         def gate_made(h):
@@ -252,48 +258,45 @@ def tile_list_hwayt_dl_silu_kernel(
                     gated[h][:, cols], gate_tanh[:, h, cols], 1.0, made[:, h, cols], ALU.add, ALU.mult
                 )
 
-        gate_made(0)
-
-        def turn(bank, source, j0, j1, start, stop):
-            for j in range(j0, j1, P):
-                nc.tensor.matmul(
-                    bank[:, j - j0 : j - j0 + P],
-                    source[:, j : j + P],
-                    identity[:],
-                    start=start and j == j0,
-                    stop=stop and j == j1 - P,
-                    is_transpose=True,
-                )
-
-        pieces = [(h, j0, j1) for h in range(HALVES) for j0, j1 in zip(TENSOR_CUTS[h], TENSOR_CUTS[h][1:])]
-        sums = []
-        for (h, j0, j1), tag in zip(pieces, ("hid10", "hid11")):
-            bank = psum.tile([P, BANK], F32, name=f"sum{h}{j0}", tag=tag)
-            turn(bank, gated[h], j0, j1, True, False)
-            sums.append(bank)
-
         def keep_carried(h, j0, j1):
             nc.vector.tensor_tensor(
                 kept[:, h, j0:j1], carried[h][:].indirect(listed(j0, j1)), carry_gate[h][:, j0:j1], ALU.mult
             )
 
-        for (h, j0, j1), bank, tag, queue in zip(pieces, sums, ("hid00", "hid01"), (nc.sync, nc.scalar)):
-            keep_carried(h, j0, j1)
-            turn(bank, kept[:, h, :], j0, j1, False, True)
-            nc.scalar.copy(turned[:, h, j0:j1], bank[:, : j1 - j0])
-            back = psum.tile([P, BANK], F32, name=f"back{h}{j0}", tag=tag)
-            turn(back, turned[:, h, :], j0, j1, True, True)
-            nc.scalar.activation(result[:, h, j0:j1], back[:, : j1 - j0], ACT.Copy, scale=0.5)
-            queue.dma_start(out[h * P : (h + 1) * P, j0:j1], result[:, h, j0:j1])
-
-        h = HALVES - 1
-        gate_made(h)
-        for step in range(len(VECTOR_CUTS)):
-            if step < len(VECTOR_CUTS) - 1:
-                keep_carried(h, VECTOR_CUTS[step], VECTOR_CUTS[step + 1])
-            if step > 0:
-                j0, j1 = VECTOR_CUTS[step - 1], VECTOR_CUTS[step]
-                nc.vector.scalar_tensor_tensor(
-                    result[:, h, j0:j1], gated[h][:, j0:j1], 0.5, kept[:, h, j0:j1], ALU.mult, ALU.add
+        def turn(bank, source, b, start, stop):
+            for c in range(0, BANK, P):
+                nc.tensor.matmul(
+                    bank[:, c : c + P],
+                    source[:, b * BANK + c : b * BANK + c + P],
+                    identity[:],
+                    start=start and c == 0,
+                    stop=stop and c == BANK - P,
+                    is_transpose=True,
                 )
-                nc.sync.dma_start(out[h * P : (h + 1) * P, j0:j1], result[:, h, j0:j1])
+
+        gate_made(0)
+        sums = []
+        for b in range(BANKS):
+            bank = psum.tile([P, BANK], F32, name=f"sum0{b * BANK}", tag=f"hid1{b}")
+            turn(bank, gated[0], b, True, False)
+            sums.append(bank)
+        for b, queue in enumerate((nc.sync, nc.scalar)):
+            cols = slice(b * BANK, (b + 1) * BANK)
+            keep_carried(0, cols.start, cols.stop)
+            turn(sums[b], kept[:, 0, :], b, False, True)
+            nc.scalar.copy(turned[:, cols], sums[b][:])
+            back = psum.tile([P, BANK], F32, name=f"back0{b * BANK}", tag=f"hid0{b}")
+            turn(back, turned, b, True, True)
+            nc.scalar.activation(result[:, 0, cols], back[:], ACT.Copy, scale=0.5)
+            queue.dma_start(out[:P, cols], result[:, 0, cols])
+
+        gate_made(1)
+        pieces = list(zip(LAST_CUTS, LAST_CUTS[1:]))
+        keep_carried(1, *pieces[0])
+        for step, (j0, j1) in enumerate(pieces):
+            if step + 1 < len(pieces):
+                keep_carried(1, *pieces[step + 1])
+            nc.vector.scalar_tensor_tensor(
+                result[:, 1, j0:j1], gated[1][:, j0:j1], 0.5, kept[:, 1, j0:j1], ALU.mult, ALU.add
+            )
+            nc.sync.dma_start(out[P:, j0:j1], result[:, 1, j0:j1])

@@ -45,28 +45,28 @@ def tile_list_hwayt_dl_silu_kernel(
 
         fp4_words = []
         for name, words in (("wg", wg_words), ("wh4", wh4_words)):
-            tile = keep.tile([P, PASSES, 2 * N], U8, name=name, align_bytes=64)
+            tile = keep.tile([P, PASSES, 2 * N], U8, name=name, align_bytes=256)
             nc.sync.dma_start(tile[:].bitcast(I32), words.rearrange("a p n -> p a n").bitcast(I32))
             fp4_words.append(tile)
 
-        offsets = keep.tile([P, J // GROUP], U16, name="offsets")
+        offsets = keep.tile([P, J // GROUP], U16, name="offsets", align_bytes=256)
         nc.sync.dma_start(offsets[:], offs)
 
         def listed(j0, j1):
             return offsets[:, j0 // GROUP : j1 // GROUP]
 
         windows = [
-            keep.tile([P, T // 4], I32, name="window0", align_bytes=64),
-            arena.tile([P, T // 4], I32, name="window1", offset=SECOND_WINDOW, align_bytes=64),
+            keep.tile([P, T // 4], I32, name="window0", align_bytes=256),
+            arena.tile([P, T // 4], I32, name="window1", offset=SECOND_WINDOW, align_bytes=256),
         ]
         for window in windows:
             nc.vector.memset(window[:], 0)
-        early_planes = keep.tile([P, (2 * W_BYTES + J) // 4], I32, name="early_plane", align_bytes=64)
-        late_planes = keep.tile([P, 2 * J // 4], I32, name="late_plane", align_bytes=64)
+        early_planes = keep.tile([P, (2 * W_BYTES + J) // 4], I32, name="early_plane", align_bytes=256)
+        late_planes = keep.tile([P, 2 * J // 4], I32, name="late_plane", align_bytes=256)
         for planes in (early_planes, late_planes):
             nc.vector.memset(planes[:], 0)
 
-        staged = keep.tile([P, (2 * W_BYTES + 2 * J) // 4], I32, name="staged", align_bytes=64)
+        staged = keep.tile([P, (2 * W_BYTES + 2 * J) // 4], I32, name="staged", align_bytes=256)
         for w, scales in enumerate((wg_scales, wh4_scales)):
             c0 = w * W_BYTES // 4
             nc.sync.dma_start(
@@ -81,16 +81,16 @@ def tile_list_hwayt_dl_silu_kernel(
         nc.scalar.activation(warm_up[:], identity[:, 0:2], ACT.Silu)
 
         def load_table(a):
-            words = arena.tile([P, T], I32, name=f"table{a}", offset=a * AREA, align_bytes=64)
+            words = arena.tile([P, T], I32, name=f"table{a}", offset=a * AREA, align_bytes=256)
             nc.sync.dma_start(words[:], tab_words[a].rearrange("p t i -> p (t i)").bitcast(I32))
             return words
 
         def load_whd(a0, a1, offset):
-            raw = arena.tile([P, a1 - a0, 4, N], F32, name=f"whd_raw{a0}", offset=offset, align_bytes=64)
+            raw = arena.tile([P, a1 - a0, 4, N], F32, name=f"whd_raw{a0}", offset=offset, align_bytes=256)
             nc.sync.dma_start(raw[:], whd[512 * a0 : 512 * a1, :].rearrange("(a p i) n -> p a i n", p=P, i=4))
             return [raw[:, a] for a in range(a1 - a0)]
 
-        bias_rows = keep.tile([P, P], F32, name="bias_rows")
+        bias_rows = keep.tile([P, P], F32, name="bias_rows", align_bytes=256)
         nc.sync.dma_start(bias_rows[P - HALVES :, :], bg.rearrange("(h p) -> h p", p=P))
         nc.sync.dma_start(windows[0][32:96:2, :], tab_scales[0:2].rearrange("a q t -> q a t").bitcast(I32))
         tables = [load_table(0)]
@@ -104,7 +104,7 @@ def tile_list_hwayt_dl_silu_kernel(
         nc.scalar.activation(half_bias[:], bias_turned[:, P - HALVES : P], ACT.Copy, scale=0.5)
 
         for g, (planes, row0, first_word) in enumerate(((early_planes, 32, 0), (late_planes, 34, 2 * W_BYTES // 4))):
-            picked_scales = arena.tile([P, J], U8, name=f"picked_scales{g}", offset=(g + 1) * AREA, align_bytes=64)
+            picked_scales = arena.tile([P, J], U8, name=f"picked_scales{g}", offset=(g + 1) * AREA, align_bytes=256)
             for b in range(BANKS):
                 nc.vector.tensor_copy(
                     picked_scales[:, b * BANK : (b + 1) * BANK],
@@ -136,8 +136,8 @@ def tile_list_hwayt_dl_silu_kernel(
             for h in range(HALVES)
         ]
 
-        picked_words = [arena.tile([P, J], U32, name="picked0", offset=SECOND_WINDOW, align_bytes=64)]
-        picked_words.extend(keep.tile([P, J], U32, name=f"picked{a}", align_bytes=64) for a in range(1, PASSES))
+        picked_words = [arena.tile([P, J], U32, name="picked0", offset=SECOND_WINDOW, align_bytes=256)]
+        picked_words.extend(keep.tile([P, J], U32, name=f"picked{a}", align_bytes=256) for a in range(1, PASSES))
 
         def multiply(acc, lhsT, lhsT_scale, a, b, start, stop):
             nc.tensor.matmul_mx(
@@ -157,13 +157,13 @@ def tile_list_hwayt_dl_silu_kernel(
 
         whd_bf16 = dict()
         whd_codes = [
-            arena.tile([P, PASSES, P], U32, name=f"whd_codes{h}", offset=GATES + 4 * J * h, align_bytes=64)
+            arena.tile([P, PASSES, P], U32, name=f"whd_codes{h}", offset=GATES + 4 * J * h, align_bytes=256)
             for h in range(HALVES)
         ]
-        whd_scales = keep.tile([P, PASSES, N], U8, name="whd_scales", align_bytes=64)
+        whd_scales = keep.tile([P, PASSES, N], U8, name="whd_scales", align_bytes=256)
 
         def interleave_whd(copy, a, h, tag):
-            tile = keep.tile([P, P, 4], BF16, name=f"whd_bf16{a}{h}", tag=tag, align_bytes=64)
+            tile = keep.tile([P, P, 4], BF16, name=f"whd_bf16{a}{h}", tag=tag, align_bytes=256)
             copy(
                 tile[:].rearrange("p (c n) i -> p c i n", n=4),
                 whd_raw[a][:, :, h * P : (h + 1) * P].rearrange("p i (c n) -> p c i n", n=4),
@@ -207,13 +207,13 @@ def tile_list_hwayt_dl_silu_kernel(
         whd_raw.extend(load_whd(1, PASSES, 0))
         carried = []
         for h in range(HALVES):
-            rows = arena.tile([P, T], F32, name=f"carried{h}", offset=(h + 1) * AREA, align_bytes=64)
+            rows = arena.tile([P, T], F32, name=f"carried{h}", offset=(h + 1) * AREA, align_bytes=256)
             nc.sync.dma_start(rows[:], rT[h * P : (h + 1) * P, :])
             carried.append(rows)
 
         gate_tanh = keep.tile([P, HALVES, J], F32, name="gate_tanh")
         carry_gate = [
-            arena.tile([P, J], F32, name=f"carry_gate{h}", offset=GATES + 4 * J * h, align_bytes=64)
+            arena.tile([P, J], F32, name=f"carry_gate{h}", offset=GATES + 4 * J * h, align_bytes=256)
             for h in range(HALVES)
         ]
 
@@ -245,11 +245,11 @@ def tile_list_hwayt_dl_silu_kernel(
 
         gated = [
             keep.tile([P, J], F32, name="gated0"),
-            arena.tile([P, J], F32, name="gated1", offset=AREA, align_bytes=64),
+            arena.tile([P, J], F32, name="gated1", offset=AREA, align_bytes=256),
         ]
         kept = keep.tile([P, HALVES, J], F32, name="kept")
         turned = keep.tile([P, J], F32, name="turned")
-        result = keep.tile([P, HALVES, J], F32, name="result")
+        result = keep.tile([P, HALVES, J], F32, name="result", align_bytes=256)
 
         def gate_made(h):
             for b in range(BANKS):

@@ -31,6 +31,7 @@ GATES = FIRST_WHD + 4 * 4 * N
 SECOND_WINDOW = GATES + HALVES * 4 * J
 
 LAST_CUTS = (0, 320, 640, 896, 1024)
+FIRST_CUTS = (0, 512, 768, 896, 1024)
 
 
 def tile_list_hwayt_dl_silu_kernel(
@@ -263,32 +264,35 @@ def tile_list_hwayt_dl_silu_kernel(
                 kept[:, h, j0:j1], carried[h][:].indirect(listed(j0, j1)), carry_gate[h][:, j0:j1], ALU.mult
             )
 
-        def turn(bank, source, b, start, stop):
-            for c in range(0, BANK, P):
+        def turn(bank, source, j0, j1, start, stop):
+            for c in range(j0, j1, P):
                 nc.tensor.matmul(
-                    bank[:, c : c + P],
-                    source[:, b * BANK + c : b * BANK + c + P],
+                    bank[:, c - j0 : c - j0 + P],
+                    source[:, c : c + P],
                     identity[:],
-                    start=start and c == 0,
-                    stop=stop and c == BANK - P,
+                    start=start and c == j0,
+                    stop=stop and c == j1 - P,
                     is_transpose=True,
                 )
 
         gate_made(0)
+        pieces = list(zip(FIRST_CUTS, FIRST_CUTS[1:]))
         sums = []
-        for b in range(BANKS):
-            bank = psum.tile([P, BANK], F32, name=f"sum0{b * BANK}", tag=f"hid1{b}")
-            turn(bank, gated[0], b, True, False)
+        for step, (j0, j1) in enumerate(pieces):
+            bank = psum.tile([P, BANK], F32, name=f"sum{step}", tag=("hid10", "hid11", "gate10", "gate11")[step])
+            if step < BANKS:
+                turn(bank, gated[0], j0, j1, True, False)
             sums.append(bank)
-        for b, queue in enumerate((nc.sync, nc.scalar)):
-            cols = slice(b * BANK, (b + 1) * BANK)
-            keep_carried(0, cols.start, cols.stop)
-            turn(sums[b], kept[:, 0, :], b, False, True)
-            nc.scalar.copy(turned[:, cols], sums[b][:])
-            back = psum.tile([P, BANK], F32, name=f"back0{b * BANK}", tag=f"hid0{b}")
-            turn(back, turned, b, True, True)
-            nc.scalar.activation(result[:, 0, cols], back[:], ACT.Copy, scale=0.5)
-            queue.dma_start(out[:P, cols], result[:, 0, cols])
+        for step, (j0, j1) in enumerate(pieces):
+            keep_carried(0, j0, j1)
+            turn(sums[step], kept[:, 0, :], j0, j1, step >= BANKS, step < BANKS)
+            if step >= BANKS:
+                turn(sums[step], gated[0], j0, j1, False, True)
+            nc.scalar.copy(turned[:, j0:j1], sums[step][:, : j1 - j0])
+            back = psum.tile([P, BANK], F32, name=f"back{step}", tag=("hid00", "hid01", "gate00", "gate01")[step])
+            turn(back, turned, j0, j1, True, True)
+            nc.scalar.activation(result[:, 0, j0:j1], back[:, : j1 - j0], ACT.Copy, scale=0.5)
+            (nc.sync if j1 < J else nc.scalar).dma_start(out[:P, j0:j1], result[:, 0, j0:j1])
 
         gate_made(1)
         pieces = list(zip(LAST_CUTS, LAST_CUTS[1:]))

@@ -70,7 +70,7 @@ def tile_list_hwayt_dl_silu_kernel(
         staged = keep.tile([P, (2 * W_BYTES + 2 * J) // 4], I32, name="staged", align_bytes=256)
         for w, scales in enumerate((wg_scales, wh4_scales)):
             c0 = w * W_BYTES // 4
-            nc.sync.dma_start(
+            nc.scalar.dma_start(
                 staged[32:96:4, c0 : c0 + W_BYTES // 4].rearrange("q (a n) -> q a n", a=PASSES),
                 scales.rearrange("a q n -> q a n").bitcast(I32),
             )
@@ -92,7 +92,7 @@ def tile_list_hwayt_dl_silu_kernel(
             return [raw[:, a] for a in range(a1 - a0)]
 
         bias_rows = keep.tile([P, P], F32, name="bias_rows", align_bytes=256)
-        nc.sync.dma_start(bias_rows[P - HALVES :, :], bg.rearrange("(h p) -> h p", p=P))
+        nc.scalar.dma_start(bias_rows[P - HALVES :, :], bg.rearrange("(h p) -> h p", p=P))
         nc.sync.dma_start(windows[0][32:96:2, :], tab_scales[0:2].rearrange("a q t -> q a t").bitcast(I32))
         tables = [load_table(0)]
         nc.sync.dma_start(windows[1][34:96:4, :], tab_scales[2].bitcast(I32))
@@ -164,9 +164,9 @@ def tile_list_hwayt_dl_silu_kernel(
         whd_scales = keep.tile([P, PASSES, N], U8, name="whd_scales", align_bytes=256)
 
         def interleave_whd(copy, a, h, tag):
-            tile = keep.tile([P, P, 4], BF16, name=f"whd_bf16{a}{h}", tag=tag, align_bytes=256)
+            tile = keep.tile([P, 2 * P, 4], BF16, name=f"whd_bf16{a}{h}", tag=tag, align_bytes=256)[:, :P, :]
             copy(
-                tile[:].rearrange("p (c n) i -> p c i n", n=4),
+                tile.rearrange("p (c n) i -> p c i n", n=4),
                 whd_raw[a][:, :, h * P : (h + 1) * P].rearrange("p i (c n) -> p c i n", n=4),
             )
             whd_bf16.setdefault((a, h), tile)
@@ -175,7 +175,7 @@ def tile_list_hwayt_dl_silu_kernel(
             nc.vector.quantize_mx(
                 out=whd_codes[h][:, a, :].bitcast(FP8X4),
                 scales=whd_scales[:, a, h * P : (h + 1) * P],
-                in_=whd_bf16[a, h][:].rearrange("p n i -> p (n i)"),
+                in_=whd_bf16[a, h].rearrange("p n i -> p (n i)"),
             )
 
         def multiply_whd(a, h, b, stop):
@@ -213,10 +213,7 @@ def tile_list_hwayt_dl_silu_kernel(
             carried.append(rows)
 
         gate_tanh = keep.tile([P, HALVES, J], F32, name="gate_tanh")
-        carry_gate = [
-            arena.tile([P, J], F32, name=f"carry_gate{h}", offset=GATES + 4 * J * h, align_bytes=256)
-            for h in range(HALVES)
-        ]
+        second_carry = arena.tile([P, J], F32, name="second_carry", offset=GATES + 4 * J, align_bytes=256)
 
         for h in range(HALVES):
             for a in range(1, PASSES):
@@ -225,7 +222,7 @@ def tile_list_hwayt_dl_silu_kernel(
                 quantise_whd(a, h)
 
         made = keep.tile([P, HALVES, J], F32, name="made")
-        for h, factor in enumerate((1.0, 0.5)):
+        for h in range(HALVES):
             for b in range(BANKS):
                 cols = slice(b * BANK, (b + 1) * BANK)
                 nc.scalar.activation(
@@ -238,15 +235,21 @@ def tile_list_hwayt_dl_silu_kernel(
                     multiply_fp4(1, hidden_sum[h][b], last_pass, h, b, False, True)
             for b in range(BANKS):
                 nc.scalar.activation(made[:, h, b * BANK : (b + 1) * BANK], hidden_sum[h][b][:], ACT.Silu)
-            for b in range(BANKS):
-                cols = slice(b * BANK, (b + 1) * BANK)
-                nc.scalar.activation(
-                    carry_gate[h][:, cols], gate_tanh[:, h, cols], ACT.Copy, scale=-factor, bias=factor
-                )
+            if h == 0:
+                first_carry = [
+                    keep.tile([P, BANK], F32, name=f"first_carry{b}", tag=f"late{b}", align_bytes=256)
+                    for b in range(BANKS)
+                ]
+                for b in range(BANKS):
+                    cols = slice(b * BANK, (b + 1) * BANK)
+                    nc.vector.tensor_scalar(first_carry[b][:], gate_tanh[:, 0, cols], -1.0, 1.0, ALU.mult, ALU.add)
+        for b in range(BANKS):
+            cols = slice(b * BANK, (b + 1) * BANK)
+            nc.scalar.activation(second_carry[:, cols], gate_tanh[:, 1, cols], ACT.Copy, scale=-0.5, bias=0.5)
 
         gated = [
             keep.tile([P, J], F32, name="gated0"),
-            arena.tile([P, J], F32, name="gated1", offset=AREA, align_bytes=256),
+            keep.tile([P, J], F32, name="gated1", tag="late0", align_bytes=256),
         ]
         kept = keep.tile([P, HALVES, J], F32, name="kept")
         turned = keep.tile([P, J], F32, name="turned")
@@ -260,9 +263,8 @@ def tile_list_hwayt_dl_silu_kernel(
                 )
 
         def keep_carried(h, j0, j1):
-            nc.vector.tensor_tensor(
-                kept[:, h, j0:j1], carried[h][:].indirect(listed(j0, j1)), carry_gate[h][:, j0:j1], ALU.mult
-            )
+            carry = second_carry[:, j0:j1] if h else first_carry[j0 // BANK][:, j0 % BANK : j0 % BANK + j1 - j0]
+            nc.vector.tensor_tensor(kept[:, h, j0:j1], carried[h][:].indirect(listed(j0, j1)), carry, ALU.mult)
 
         def turn(bank, source, j0, j1, start, stop):
             for c in range(j0, j1, P):

@@ -118,7 +118,9 @@ def tile_list_hwayt_dl_silu_kernel(
                 )
             for r in range(4):
                 nc.sync.dma_start(
-                    planes[r:P:32, :], staged[row0 + 4 * r : 96 : 16, first_word : first_word + planes.shape[1]]
+                    planes[r:P:32, :],
+                    staged[row0 + 4 * r : 96 : 16, first_word : first_word + planes.shape[1]],
+                    max_dma_last_dim=512,
                 )
             tables.append(load_table(g + 1))
         weight_planes = early_planes[:, : 2 * W_BYTES // 4].bitcast(U8)

from contextlib import ExitStack

import concourse.mybir as mybir
from concourse.masks import make_identity

K, N, T, J = 1536, 256, 4096, 1024
FLOPS = 3 * 2 * K * N * J

F32 = mybir.dt.float32
BF16 = mybir.dt.bfloat16
I32 = mybir.dt.int32
U32 = mybir.dt.uint32
U16 = mybir.dt.uint16
U8 = mybir.dt.uint8
FP8X4 = mybir.dt.float8_e4m3fn_x4
FP4X4 = mybir.dt.float4_e2m1fn_x4
ALU = mybir.AluOpType
ACT = mybir.ActivationFunctionType

P = 128
PASSES = K // 512
HALVES = N // P
BANK = 512
BANKS = J // BANK
GROUP = 16
W_BYTES = PASSES * N

AREA = 4 * T
FIRST_WHD = 3 * AREA
GATES = FIRST_WHD + 4 * 4 * N
SECOND_WINDOW = GATES + HALVES * 4 * J

LAST_CUTS = (0, 320, 640, 896, 1024)
FIRST_CUTS = (0, 512, 768, 896, 1024)


def tile_list_hwayt_dl_silu_kernel(
    tc, tab_words, tab_scales, wg_words, wg_scales, wh4_words, wh4_scales, whd, bg, rT, offs, out
):
    nc = tc.nc

    with ExitStack() as ctx:
        keep = ctx.enter_context(tc.tile_pool(name="keep", bufs=1))
        arena = ctx.enter_context(tc.tile_pool(name="arena", bufs=1))
        psum = ctx.enter_context(tc.psum_pool(name="psum", bufs=1))

        fp4_words = []
        for name, words in (("wg", wg_words), ("wh4", wh4_words)):
            tile = keep.tile([P, PASSES, 2 * N], U8, name=name, align_bytes=256)
            nc.sync.dma_start(tile[:].bitcast(I32), words.rearrange("a p n -> p a n").bitcast(I32))
            fp4_words.append(tile)

        offsets = keep.tile([P, J // GROUP], U16, name="offsets", align_bytes=256)
        nc.sync.dma_start(offsets[:], offs)

        def listed(j0, j1):
            return offsets[:, j0 // GROUP : j1 // GROUP]

        windows = [
            keep.tile([P, T // 4], I32, name="window0", align_bytes=256),
            arena.tile([P, T // 4], I32, name="window1", offset=SECOND_WINDOW, align_bytes=256),
        ]
        for window in windows:
            nc.vector.memset(window[:], 0)
        early_planes = keep.tile([P, (2 * W_BYTES + J) // 4], I32, name="early_plane", align_bytes=256)
        late_planes = keep.tile([P, 2 * J // 4], I32, name="late_plane", align_bytes=256)
        for planes in (early_planes, late_planes):
            nc.vector.memset(planes[:], 0)

        staged = keep.tile([P, (2 * W_BYTES + 2 * J) // 4], I32, name="staged", align_bytes=256)
        for w, scales in enumerate((wg_scales, wh4_scales)):
            c0 = w * W_BYTES // 4
            nc.scalar.dma_start(
                staged[32:96:4, c0 : c0 + W_BYTES // 4].rearrange("q (a n) -> q a n", a=PASSES),
                scales.rearrange("a q n -> q a n").bitcast(I32),
            )

        identity = keep.tile([P, P], F32, name="identity")
        nc.vector.memset(identity[:], 0.0)
        make_identity(nc, identity[:], nomemset=True)
        warm_up = keep.tile([P, 2], F32, name="warm_up")
        nc.scalar.activation(warm_up[:], identity[:, 0:2], ACT.Silu)

        def load_table(a):
            words = arena.tile([P, T], I32, name=f"table{a}", offset=a * AREA, align_bytes=256)
            nc.sync.dma_start(words[:], tab_words[a].rearrange("p t i -> p (t i)").bitcast(I32))
            return words

        def load_whd(a0, a1, offset):
            raw = arena.tile([P, a1 - a0, 4, N], F32, name=f"whd_raw{a0}", offset=offset, align_bytes=256)
            nc.sync.dma_start(raw[:], whd[512 * a0 : 512 * a1, :].rearrange("(a p i) n -> p a i n", p=P, i=4))
            return [raw[:, a] for a in range(a1 - a0)]

        bias_rows = keep.tile([P, P], F32, name="bias_rows", align_bytes=256)
        nc.scalar.dma_start(bias_rows[P - HALVES :, :], bg.rearrange("(h p) -> h p", p=P))
        nc.sync.dma_start(windows[0][32:96:2, :], tab_scales[0:2].rearrange("a q t -> q a t").bitcast(I32))
        tables = [load_table(0)]
        nc.sync.dma_start(windows[1][34:96:4, :], tab_scales[2].bitcast(I32))
        whd_raw = load_whd(0, 1, FIRST_WHD)

        nc.vector.memset(bias_rows[: P - HALVES, :], 0.0)
        bias_turned = psum.tile([P, BANK], F32, name="bias_turned", tag="hid11")
        nc.tensor.transpose(bias_turned[:, :P], bias_rows[:], identity[:])
        half_bias = keep.tile([P, HALVES], F32, name="half_bias")
        nc.scalar.activation(half_bias[:], bias_turned[:, P - HALVES : P], ACT.Copy, scale=0.5)

        for g, (planes, row0, first_word) in enumerate(((early_planes, 32, 0), (late_planes, 34, 2 * W_BYTES // 4))):
            picked_scales = arena.tile([P, J], U8, name=f"picked_scales{g}", offset=(g + 1) * AREA, align_bytes=256)
            for b in range(BANKS):
                nc.vector.tensor_copy(
                    picked_scales[:, b * BANK : (b + 1) * BANK],
                    windows[g][:].bitcast(U8).indirect(listed(b * BANK, (b + 1) * BANK)),
                )
            for b in range(BANKS):
                c0 = (2 * W_BYTES + g * J + b * BANK) // 4
                nc.vector.tensor_copy(
                    staged[:, c0 : c0 + BANK // 4], picked_scales[:, b * BANK : (b + 1) * BANK].bitcast(I32)
                )
            for r in range(4):
                nc.sync.dma_start(
                    planes[r:P:32, :],
                    staged[row0 + 4 * r : 96 : 16, first_word : first_word + planes.shape[1]],
                    max_dma_last_dim=512,
                )
            tables.append(load_table(g + 1))
        weight_planes = early_planes[:, : 2 * W_BYTES // 4].bitcast(U8)
        table_planes = [
            early_planes[:, 2 * W_BYTES // 4 :].bitcast(U8),
            late_planes[:, : J // 4].bitcast(U8),
            late_planes[:, J // 4 :].bitcast(U8),
        ]

        gate_sum = [
            [psum.tile([P, BANK], F32, name=f"gate{h}{b}", tag=f"gate{h}{b}") for b in range(BANKS)]
            for h in range(HALVES)
        ]
        hidden_sum = [
            [psum.tile([P, BANK], F32, name=f"hid{h}{b}", tag=f"hid{h}{b}") for b in range(BANKS)]
            for h in range(HALVES)
        ]

        picked_words = [arena.tile([P, J], U32, name="picked0", offset=SECOND_WINDOW, align_bytes=256)]
        picked_words.extend(keep.tile([P, J], U32, name=f"picked{a}", align_bytes=256) for a in range(1, PASSES))

        def multiply(acc, lhsT, lhsT_scale, a, b, start, stop):
            nc.tensor.matmul_mx(
                out=acc[:],
                lhsT=lhsT,
                lhsT_scale=lhsT_scale,
                rhs=picked_words[a][:, b * BANK : (b + 1) * BANK].bitcast(FP8X4),
                rhs_scale=table_planes[a][:, b * BANK : (b + 1) * BANK],
                start=start,
                stop=stop,
            )

        def multiply_fp4(w, acc, a, h, b, start, stop):
            c0 = w * W_BYTES + a * N + h * P
            codes = fp4_words[w][:, a, 2 * h * P : 2 * (h + 1) * P].bitcast(FP4X4)
            multiply(acc, codes, weight_planes[:, c0 : c0 + P], a, b, start, stop)

        whd_bf16 = dict()
        whd_codes = [
            arena.tile([P, PASSES, P], U32, name=f"whd_codes{h}", offset=GATES + 4 * J * h, align_bytes=256)
            for h in range(HALVES)
        ]
        whd_scales = keep.tile([P, PASSES, N], U8, name="whd_scales", align_bytes=256)

        def interleave_whd(copy, a, h, tag):
            tile = keep.tile([P, 2 * P, 4], BF16, name=f"whd_bf16{a}{h}", tag=tag, align_bytes=256)[:, :P, :]
            copy(
                tile.rearrange("p (c n) i -> p c i n", n=4),
                whd_raw[a][:, :, h * P : (h + 1) * P].rearrange("p i (c n) -> p c i n", n=4),
            )
            whd_bf16.setdefault((a, h), tile)

        def quantise_whd(a, h):
            nc.vector.quantize_mx(
                out=whd_codes[h][:, a, :].bitcast(FP8X4),
                scales=whd_scales[:, a, h * P : (h + 1) * P],
                in_=whd_bf16[a, h].rearrange("p n i -> p (n i)"),
            )

        def multiply_whd(a, h, b, stop):
            codes = whd_codes[h][:, a, :].bitcast(FP8X4)
            multiply(hidden_sum[h][b], codes, whd_scales[:, a, h * P : (h + 1) * P], a, b, False, stop)

        for h in range(HALVES):
            interleave_whd(nc.scalar.copy, 0, h, f"early{h}")

        last_pass = PASSES - 1
        for a in range(PASSES):
            for b in range(BANKS):
                nc.vector.tensor_copy(
                    picked_words[a][:, b * BANK : (b + 1) * BANK],
                    tables[a][:].bitcast(U32).indirect(listed(b * BANK, (b + 1) * BANK)),
                )
            for b in range(BANKS):
                for h in range(HALVES):
                    multiply_fp4(0, gate_sum[h][b], a, h, b, a == 0, a == last_pass)
                for h in range(HALVES if a < last_pass else 1):
                    multiply_fp4(1, hidden_sum[h][b], a, h, b, a == 0, False)
            if a == 0:
                for h in range(HALVES):
                    quantise_whd(0, h)
            if a == last_pass - 1:
                for h in range(HALVES):
                    for b in range(BANKS):
                        multiply_whd(0, h, b, False)

        whd_raw.extend(load_whd(1, PASSES, 0))
        carried = []
        for h in range(HALVES):
            rows = arena.tile([P, T], F32, name=f"carried{h}", offset=(h + 1) * AREA, align_bytes=256)
            nc.sync.dma_start(rows[:], rT[h * P : (h + 1) * P, :])
            carried.append(rows)

        gate_tanh = keep.tile([P, HALVES, J], F32, name="gate_tanh")
        second_carry = arena.tile([P, J], F32, name="second_carry", offset=GATES + 4 * J, align_bytes=256)

        for h in range(HALVES):
            for a in range(1, PASSES):
                interleave_whd(nc.vector.tensor_copy, a, h, f"late{(a + h) % 2}")
            for a in range(1, PASSES):
                quantise_whd(a, h)

        made = keep.tile([P, HALVES, J], F32, name="made")
        for h in range(HALVES):
            for b in range(BANKS):
                cols = slice(b * BANK, (b + 1) * BANK)
                nc.scalar.activation(
                    gate_tanh[:, h, cols], gate_sum[h][b][:], ACT.Tanh, bias=half_bias[:, h : h + 1], scale=0.5
                )
            for b in range(BANKS):
                for a in range(1, PASSES):
                    multiply_whd(a, h, b, h == 0 and a == last_pass)
                if h == 1:
                    multiply_fp4(1, hidden_sum[h][b], last_pass, h, b, False, True)
            for b in range(BANKS):
                nc.scalar.activation(made[:, h, b * BANK : (b + 1) * BANK], hidden_sum[h][b][:], ACT.Silu)
            if h == 0:
                first_carry = [
                    keep.tile([P, BANK], F32, name=f"first_carry{b}", tag=f"late{b}", align_bytes=256)
                    for b in range(BANKS)
                ]
                for b in range(BANKS):
                    cols = slice(b * BANK, (b + 1) * BANK)
                    nc.vector.tensor_scalar(first_carry[b][:], gate_tanh[:, 0, cols], -1.0, 1.0, ALU.mult, ALU.add)
        for b in range(BANKS):
            cols = slice(b * BANK, (b + 1) * BANK)
            nc.scalar.activation(second_carry[:, cols], gate_tanh[:, 1, cols], ACT.Copy, scale=-0.5, bias=0.5)

        gated = [
            keep.tile([P, J], F32, name="gated0"),
            keep.tile([P, J], F32, name="gated1", tag="late0", align_bytes=256),
        ]
        kept = keep.tile([P, HALVES, J], F32, name="kept")
        turned = keep.tile([P, J], F32, name="turned")
        result = keep.tile([P, HALVES, J], F32, name="result", align_bytes=256)

        def gate_made(h):
            for b in range(BANKS):
                cols = slice(b * BANK, (b + 1) * BANK)
                nc.vector.scalar_tensor_tensor(
                    gated[h][:, cols], gate_tanh[:, h, cols], 1.0, made[:, h, cols], ALU.add, ALU.mult
                )

        def keep_carried(h, j0, j1):
            carry = second_carry[:, j0:j1] if h else first_carry[j0 // BANK][:, j0 % BANK : j0 % BANK + j1 - j0]
            nc.vector.tensor_tensor(kept[:, h, j0:j1], carried[h][:].indirect(listed(j0, j1)), carry, ALU.mult)

        def turn(bank, source, j0, j1, start, stop):
            for c in range(j0, j1, P):
                nc.tensor.matmul(
                    bank[:, c - j0 : c - j0 + P],
                    source[:, c : c + P],
                    identity[:],
                    start=start and c == j0,
                    stop=stop and c == j1 - P,
                    is_transpose=True,
                )

        gate_made(0)
        pieces = list(zip(FIRST_CUTS, FIRST_CUTS[1:]))
        sums = []
        for step, (j0, j1) in enumerate(pieces):
            bank = psum.tile([P, BANK], F32, name=f"sum{step}", tag=("hid10", "hid11", "gate10", "gate11")[step])
            if step < BANKS:
                turn(bank, gated[0], j0, j1, True, False)
            sums.append(bank)
        for step, (j0, j1) in enumerate(pieces):
            keep_carried(0, j0, j1)
            turn(sums[step], kept[:, 0, :], j0, j1, step >= BANKS, step < BANKS)
            if step >= BANKS:
                turn(sums[step], gated[0], j0, j1, False, True)
            nc.scalar.copy(turned[:, j0:j1], sums[step][:, : j1 - j0])
            back = psum.tile([P, BANK], F32, name=f"back{step}", tag=("hid00", "hid01", "gate00", "gate01")[step])
            turn(back, turned, j0, j1, True, True)
            nc.scalar.activation(result[:, 0, j0:j1], back[:, : j1 - j0], ACT.Copy, scale=0.5)
            (nc.sync if j1 < J else nc.scalar).dma_start(out[:P, j0:j1], result[:, 0, j0:j1])

        gate_made(1)
        pieces = list(zip(LAST_CUTS, LAST_CUTS[1:]))
        keep_carried(1, *pieces[0])
        for step, (j0, j1) in enumerate(pieces):
            if step + 1 < len(pieces):
                keep_carried(1, *pieces[step + 1])
            nc.vector.scalar_tensor_tensor(
                result[:, 1, j0:j1], gated[1][:, j0:j1], 0.5, kept[:, 1, j0:j1], ALU.mult, ALU.add
            )
            nc.sync.dma_start(out[P:, j0:j1], result[:, 1, j0:j1])
